import numpy as np, ml_dtypes
CORES = [3,11,19,27,35,43,51,59]
N = 8
BF = ml_dtypes.bfloat16
def gentries(a):
    return np.ascontiguousarray(a.reshape(8, 16, -1).transpose(0, 2, 1)).reshape(8, -1)
def gtable(e):
    e = np.asarray(e); return np.ascontiguousarray(e.reshape(8, -1, 16).transpose(0, 2, 1)).reshape(128, -1).astype(np.int32)
S, K, SH, AC, RO, Z = 2048, 4096, 3, 9, 3, 256
def one(w):
    c = np.add.accumulate(w, dtype=np.int64)
    return np.searchsorted(K * c, np.arange(K) * c[-1], side="right")
def ancestors(x, y, e):
    w = np.maximum(1, np.add.reduce(np.abs(x - y) <= e, axis=1, dtype=np.int64) >> SH)
    return np.stack([one(a) for a in w])
def parts(rng):
    fp = rng.random((N, 8, 16, S), dtype=np.float32); bp = rng.random((N, 8, 16, S), dtype=np.float32)
    nz = (rng.random((N, 8, 16, S), dtype=np.float32) - 0.5) * 0.125
    ob = 0.3 + 0.6 * rng.random((N, 8, 16, RO))
    lev = np.array([0.12, 0.18, 0.25, 0.36, 0.12, 0.18, 0.25, 0.36])[np.argsort(rng.random((N, 8)), axis=-1)][..., None]
    ep = lev * (0.7 + 0.6 * rng.random((N, 8, 16))); la = 0.2 + 0.6 * rng.random((N, 8, 16))
    r1 = 2.8 + 1.1 * rng.random((N, 8, 16)); r2 = 2.8 + 1.1 * rng.random((N, 8, 16))
    return fp, bp, nz, ob, ep, la, r1, r2, np.argsort(rng.random((N, 8, K)), axis=-1)
def pack(fp, bp, nz, ob, ep, la, r1, r2, p):
    d = {"f0": fp.reshape(N, 128, S).astype(BF), "b0": bp.reshape(N, 128, S).astype(BF), "nz": nz.reshape(N, 128, S).astype(BF), "obs": ob.reshape(N, 128, RO).astype(np.float32)}
    for k, v in (("eps", ep), ("lam", la), ("rf", r1), ("rb", r2)): d[k] = v.reshape(N, 128, 1).astype(np.float32)
    d["pi"] = np.stack([gtable(a) for a in p])
    return d
def pairing(rng, sf, sb, nand, n):
    h = max(1, AC >> SH)
    u = sf[one(np.where(sf != nand, h, 1))]; v = sb[one(np.where(sb != nand, h, 1))]
    a = rng.permutation(np.flatnonzero(u)); c = np.flatnonzero(~u); x = rng.permutation(np.flatnonzero(v)); z = rng.permutation(np.flatnonzero(~v))
    n = max(len(a) + len(x) - K, min(n, len(a), len(x))); p = np.zeros(K, np.int64)
    p[a[:n]] = x[:n]; p[a[n:]] = z[:len(a) - n]; p[c] = rng.permutation(np.concatenate([x[n:], z[len(a) - n:]]))
    return p
def setup_inputs(rng):
    return pack(*parts(rng))
def setup_inputs_spread(rng):
    fp, bp, nz, ob, ep, la, r1, r2, p = parts(rng); s = (N, 8, 1, S)
    fp = fp * np.exp2(-rng.integers(0, 4, s)) * (rng.random(s) > 0.0625); bp = bp * np.exp2(-rng.integers(0, 4, s)) * (rng.random(s) > 0.0625)
    nz = 2 * nz * np.exp2(-rng.integers(0, 4, s)) * (rng.random(s) > 0.0625)
    ob = 0.05 + 0.85 * rng.random(ob.shape); ep = np.exp2(-4 + 3 * rng.random((N, 8, 1))) * (0.7 + 0.3 * rng.random(ep.shape))
    la = rng.random(la.shape); r1 = 2 + 2 * rng.random(r1.shape); r2 = 2 + 2 * rng.random(r2.shape)
    return pack(fp, bp, nz, ob, ep, la, r1, r2, p)
def bits(rng, *s):
    return rng.integers(0, 2, s).astype(np.float32)
def setup_inputs_ends(rng):
    fp = bits(rng, N, 8, 16, S); bp = bits(rng, N, 8, 16, S); nz = 0.25 * bits(rng, N, 8, 16, S) - 0.125; ob = bits(rng, N, 8, 16, RO)
    cnt = rng.choice(np.array([7, 8, 9, 10]), (N, 8)); cnt[:, 0] = 0; cnt[:, 1] = 8; cnt[:, 2] = 9; cnt[:, 5] = 16; cnt[:, 7] = 16
    ep = (np.argsort(rng.random((N, 8, 16)), axis=-1) < cnt[..., None]).astype(np.float32)
    la = bits(rng, N, 8, 16); r1 = 4 * bits(rng, N, 8, 16); r2 = 4 * bits(rng, N, 8, 16)
    for x in (fp, bp):
        x[:, 0] = 1 - ob[:, 0, :, :1]
        for s in (0, S - 1): x[:, 0, :, s] = ob[:, 0, :, 0]
    mid = 1 + np.argsort(rng.random((N, 8, K - 2)), axis=-1); e = np.zeros((N, 8, 1), np.int64)
    p = np.concatenate([e + K - 1, mid, e], axis=2); p[:, 1::2] = p[:, 1::2, ::-1].copy()
    return pack(fp, bp, nz, ob, ep, la, r1, r2, p)
def crowd(rng):
    pools = []
    for turn in (0, 3):
        h = np.zeros((N, 8, S), np.int64)
        for q in range(N):
            for g in range(8):
                k = (g + q + turn) % 8
                if k == 0: h[q, g] = 16
                if k == 1: h[q, g] = 16; h[q, g, S - 1] = 15
                if k == 2: h[q, g] = rng.choice(np.array([0, 2 ** SH - 1, 2 ** SH, 15, 16]), S)
                if k == 3: h[q, g] = rng.integers(8, 10, S)
                if k == 4: h[q, g, 0] = 16
                if k == 6: h[q, g] = rng.integers(7, 10, S)
                if k == 7: h[q, g] = 16; h[q, g, 0] = 8
        order = np.argsort(rng.random((N, 8, 16, S), dtype=np.float32), axis=2)
        hit = rng.choice(np.array([0.375, 0.625], np.float32), (N, 8, 16, S)); miss = rng.choice(np.array([0.25, 0.75, 0.62890625], np.float32), (N, 8, 16, S))
        pools.append(np.where(order < h[:, :, None, :], hit, miss))
    return pools
def setup_inputs_corners(rng):
    fp, bp, nz, ob, ep, la, r1, r2, p = parts(rng); fp = 0.9 * fp; bp = 0.9 * bp; h = max(1, AC >> SH)
    for q in range(0, N, 2):
        for g in range(8):
            t = min(K, (0, 1, 2, K - 1, K, 2 * S - 1, 2 * S, 2 * S + 1)[(g + q) % 8]); nand = 4 * t > 3 * K; n = K - t if nand else t
            z = 3 * S // (2 * h + 3) if K <= 4 * t and not nand else S // (h + 2)
            sf = rng.permutation(S) < z; sb = rng.permutation(S) < z; m = rng.permutation(16) < AC
            fp[q, g, m] = np.where(sf, 0.625, 0.125); bp[q, g, m] = np.where(sb, 0.625, 0.125)
            ob[q, g, :, 0] = np.where(m, 0.125 if nand else 0.625, 1.0); ep[q, g] = np.where(m, 0.25 if nand else 0.125, 0.0); la[q, g] = np.where(m, 0.5, la[q, g])
            p[q, g] = pairing(rng, sf, sb, nand, n)
    cf, cb = crowd(rng)
    for q in range(1, N, 2):
        fp[q] = cf[q]; bp[q] = cb[q]; ob[q, :, :, 0] = 0.5; ep[q] = 0.125
        o = (q // 2) % 2; la[q, o::2] = 0.0; la[q, 1 - o::2] = 1.0
    return pack(fp, bp, nz, ob, ep, la, r1, r2, p)
def setup_inputs_calm(rng):
    fp, bp, nz, ob, ep, la, r1, r2, p = parts(rng); fp = 0.9 * fp; bp = 0.9 * bp; h = max(1, AC >> SH)
    r1 = 2.8 + 0.7 * rng.random(r1.shape); r2 = 2.8 + 0.7 * rng.random(r2.shape)
    m = rng.permutation(16) < AC; r1[..., m] = 0; r2[..., m] = 0
    zs = np.argsort(rng.random((N, 8, S)), axis=-1) < S // (h + 2)
    for q in range(N):
        for g in range(8):
            nand = (g // 4 + q) % 2 == 1; sf = zs[(q - 1) % N, g]; sb = zs[(q + 1) % N, (g - 1) % 8]
            nz[q, g, m] = np.where(zs[q, g], 0.125, -0.125 * rng.integers(0, 2, (AC, S)))
            fp[q, g, m] = np.where(sf, 0.125, 0.0); bp[q, g, m] = np.where(sb, 0.125, 0.0)
            ob[q, g] = np.where(m, 0.0 if nand else 0.125, 1.0)[:, None]; ep[q, g] = np.where(m, 0.0625 if nand else 0.03125, 0.0); la[q, g] = np.where(m, 0.5, la[q, g])
            p[q, g] = pairing(rng, sf, sb, nand, (g + q) % 4)
    return pack(fp, bp, nz, ob, ep, la, r1, r2, p)
def setup_inputs_rounding(rng):
    fp, bp, nz, ob, ep, la, r1, r2, p = parts(rng); ep[:] = 0.0; m = rng.permutation(16) < AC
    r1 = 2.8 + 0.7 * rng.random(r1.shape); r2 = 2.8 + 0.7 * rng.random(r2.shape); s = (N, 8, AC)
    kd = rng.permutation(np.array([0, 0, 0, 1, 1, 2, 2, 3]))[None, :, None]; none = np.float32(0)
    x, w, z = [a.astype(BF).astype(np.float32) for a in (0.1 + 0.8 * rng.random(s), 0.1 + 0.8 * rng.random(s), 0.125 * (rng.random(s) - 0.5))]
    x = np.where(kd == 3, none, x); z = np.where(kd == 3, none, z); la[:, :, m] = np.where(kd == 3, 0.0, la[:, :, m])
    e = (2.0 ** -6 + 2.0 ** -24 * rng.integers(1, 2 ** 18, s)).astype(np.float32)
    ep[:, :, m] = np.where(kd == 1, e, np.where(kd == 2, np.nextafter(e, none), none))
    fp[:, :, m] = x[..., None]; bp[:, :, m] = w[..., None]; nz[:, :, m] = z[..., None]
    j = rng.permutation(np.flatnonzero(~m))[:2]
    fp[:, :, j] = np.where(kd[..., None] < 2, np.float32(1), fp[:, :, j]); bp[:, :, j] = 0; nz[:, :, j] = 0
    la[:, :, j] = np.where(kd < 2, 0.5, la[:, :, j]); r1[:, :, j] = np.where(kd < 2, 4.0, r1[:, :, j]); r2[:, :, j] = 0
    l, u, v = [a[..., m].astype(np.float32) for a in (la, r1, r2)]
    for t in range(RO):
        if t > 0: x = np.roll(x, 1, axis=0); w = np.roll(np.roll(w, -1, axis=0), 1, axis=1)
        y = x + l * (w - x)
        ob[:, :, m, t] = np.where(kd == 3, np.exp2(-rng.integers(80, 111, s)), np.where(kd == 0, y, y - e))
        x = step(np.where(kd < 2, y, x), u, z); w = step(np.where(kd < 2, y, w), v, z)
    return pack(fp, bp, nz, ob, ep, la, r1, r2, p)
def check_ranges(d):
    bad = []
    for k, lo, hi in (("f0", 0, 1), ("b0", 0, 1), ("nz", -0.125, 0.125), ("obs", 0, 1), ("eps", 0, 1), ("lam", 0, 1), ("rf", 0, 4), ("rb", 0, 4), ("pi", 0, K - 1)):
        a = np.asarray(d[k]).astype(np.float64)
        if not (np.min(a) >= lo and np.max(a) <= hi): bad.append("range of " + k)
    x = np.stack([gentries(np.asarray(a)) for a in d["pi"]])
    if not np.array_equal(np.sort(x, axis=-1), np.broadcast_to(np.arange(K), x.shape)): bad.append("pi isn't a permutation in every group")
    return bad
def step(a, r, z):
    return np.minimum(np.maximum(r * (a - a * a) + z, np.float32(0)), np.float32(1))
def reference(f0, b0, nz, obs, eps, lam, rf, rb, pi):
    f = f0.astype(np.float32).reshape(N, 8, 16, S); b = b0.astype(np.float32).reshape(N, 8, 16, S); z = nz.astype(np.float32).reshape(N, 8, 16, S)
    y = obs.astype(np.float32).reshape(N, 8, 16, RO); e, la, r1, r2 = [a.astype(np.float32).reshape(N, 8, 16, 1) for a in (eps, lam, rf, rb)]
    pl = np.stack([gentries(a) for a in pi]).astype(np.int64); ye = []
    for t in range(RO):
        if t > 0:
            f = np.roll(f, 1, axis=0); b = np.roll(np.roll(b, -1, axis=0), 1, axis=1)
        nf, nb = [], []
        for q in range(N):
            yt = y[q, :, :, t:t + 1]; af = ancestors(f[q], yt, e[q]); ab = ancestors(b[q], yt, e[q])
            fi = np.take_along_axis(f[q], af[:, None, :], 2); bj = np.take_along_axis(b[q], np.take_along_axis(ab, pl[q], 1)[:, None, :], 2)
            m = fi + la[q] * (bj - fi)
            ok = np.add.reduce(np.abs(m - yt) <= e[q], axis=1, dtype=np.int64) >= AC
            kf = np.take_along_axis(f[q], af[:, None, ::K // S], 2); kb = np.take_along_axis(b[q], ab[:, None, ::K // S], 2)
            for g in range(8):
                w = np.flatnonzero(ok[g])[:2 * S]; u = w[0::2]; v = w[1::2]
                kf[g, :, :len(u)] = m[g][:, u]; kb[g, :, :len(v)] = m[g][:, v]
            nf.append(step(kf, r1[q], z[q])); nb.append(step(kb, r2[q], z[q]))
            if t == RO - 1:
                d = fi.astype(np.float64) - bj.astype(np.float64)
                ye.append(np.add.reduce(np.exp(-d * d).reshape(8, 16, K // Z, Z), axis=2).reshape(128, Z))
        f = np.stack(nf); b = np.stack(nb)
    return {"yf": f.reshape(N, 128, S).astype(np.float32), "yb": b.reshape(N, 128, S).astype(np.float32), "ye": np.stack(ye).astype(np.float32)}

def check_inputs(d):
    bad = list(check_ranges(d))
    if not bad:
        for name, y in reference(**d).items():
            for q in range(N):
                v = np.abs(np.asarray(y[q], np.float64))
                if v.max() > 4 * np.sqrt(np.mean(v * v)): bad.append('%s of rank %d is uneven' % (name, q))
    return bad

@@ -1,0 +1,667 @@
+import numpy as np
+from concourse.bass import DstId, RemoteDMATransfer
+from concourse.mybir import dt, AluOpType, AxisListType, ActivationFunctionType
+
+AL = AluOpType
+AF = ActivationFunctionType
+S, K, N = 2048, 4096, 8
+MG = 12582912.0
+BIG = 32768.0
+SC = 2.0 ** 60
+WM, WF, WB, WW = 8, 8 + K, 8 + 2 * K, 8 + 3 * K
+
+F, H, I, U = "float32", "bfloat16", "int32", "uint16"
+SCRATCH = {}
+for _n, _w, _d in [
+    ("f0s", S, H), ("b0s", S, H), ("nza", S, H), ("nzb", S, H), ("pis", 256, I), ("pia", 256, U), ("pib", 256, U),
+    ("pra", 8, F), ("prb", 8, F), ("pna", 8, F), ("pnb", 8, F), ("prc", 8, F), ("prd", 8, F), ("pnc", 8, F), ("pnd", 8, F),
+    ("sab", 256, U), ("saf", 256, U), ("lab", 256, U), ("laf", 256, U),
+    ("win", WW, F), ("dd", K, F), ("ab", K, F), ("tb", K, F), ("hit", K, H), ("aw", S, F), ("mw", 2 * S, H),
+    ("fp1", S, F), ("sb0", S, F), ("lb", S, F), ("sf1", S, F), ("lf", S, F), ("yes", 256, F),
+    ("zz", K, H), ("zcf", 1408, H), ("zcb", 1408, H), ("ef", 136, F), ("eg", 136, F),
+    ("iod", 144, F), ("rci", 2, I), ("rc", 4, F), ("j16", 272, F), ("dmask", 272, F), ("c16", 256, H), ("mc", 512, F),
+    ("nb16", 272, F), ("nfill", 256, F), ("tbc", 17, I), ("k16", 16, F), ("ta", 128, F), ("tc", 128, F),
+    ("q1", 144, H), ("qw", 144, H), ("qd", 144, H), ("bo", 128, H), ("bo16", 128, H), ("tri", 128, H), ("str", 128, H),
+    ("idb", 128, H), ("shb", 128, H), ("idf", 128, F), ("shf", 128, F),
+    ("ok", 256, H), ("po", 280, F), ("oi", 272, I), ("pa", 272, I), ("pg", 272, F), ("px", 256, I), ("py", 256, I),
+    ("pc", 256, H), ("pe", 544, F), ("pk", 34, I), ("pk2", 34, I), ("pq", 17, I), ("pq2", 17, I), ("pl", 18, U),
+    ("d0", 256, F), ("t1", 256, F), ("nn", 280, F), ("yy", 272, F), ("pw", 832, F), ("ll", 256, U),
+]:
+    SCRATCH[_n] = ("sbuf", [128, _w], _d)
+for _x in "fb":
+    for _n, _w, _d in [("w", 128, H), ("o", 136, F), ("tq", 4, F), ("en", 8, F), ("qm", 128, F), ("qt", 128, F), ("st", 136, F),
+                       ("ec", 128, F), ("eb", 256, F), ("l2", 32, U), ("x12", 512, H), ("p0", 256, H),
+                       ("xs", 256, H), ("al", 256, U)]:
+        SCRATCH[_n + _x] = ("sbuf", [128, _w], _d)
+PS = {"psa": (1024, 0), "psb": (1024, 2), "ps4": (512, 4), "ps5": (512, 5), "ps6": (512, 6), "ps7": (512, 7)}
+for _n in PS:
+    SCRATCH[_n] = ("psum", [128, PS[_n][0]], F)
+
+CFG = {
+    "gch": [1024, 1024, 1024, 512, 512],
+    "parts": [128, 256],
+    "sch": [[512] * 4, [512] * 4, [512, 512, 512, 256, 256]],
+    "step": ["bbbbffff", "ffffbbbb", "fbfbfbfbfb"], "sf": [0.0, 0.0, 0.0], "sb": [0.0, 0.0, 0.0], "q": "a",
+    "nzp": ["P" * 10, "P" * 10, "P" * 10],
+    "hit": {0: {"b": "AA", "f": "AA"}, 1: {"f": "AAAA", "b": "AAAA"}, 2: {"b": "AAAA", "f": "AAAA"}},
+    "order": ["bf", "bf", "fb"],
+    "bA": 4, "acc": ["AAAVV", "AAAVV", "VVVVV"], "coarse": "a", "small": "a",
+    "bb": [0.0, 0.0, 0.0], "bf": [0.0, 0.0, 0.0], "bp": 0.0,
+    "pv": 3000.0, "pa": 3000.0, "noise": 0.0, "seed": 0,
+    "g": 1.56, "sc": 3.8, "pe": 0.5, "lat": 100.0, "fix": 60.0, "link": 60.0, "nudge": {},
+}
+CFG.update({
+    'gch': [512] * 8, 'parts': [128, 256], 'sch': [[256, 512, 512, 512, 256], [512, 512, 512, 512], [512, 512, 512, 256, 256]],
+    'step': ['bfbbffbfbf', 'fbbfbbff', 'bbbfffffbb'], 'sf': [-2000.0, 2000.0, 0.0], 'sb': [-2000.0, 2000.0, 0.0], 'q': 'a',
+    'nzp': ['PPPPPPPPVP', 'PPPPPPVPPP', 'PPPPPVPPPP'],
+    'hit': {0: {'b': 'AD', 'f': 'AD'}, 1: {'f': 'AAAA', 'b': 'AA'}, 2: {'b': 'AA', 'f': 'AA'}}, 'order': ['bf', 'bf', 'fb'],
+    'bA': 2, 'acc': ['VVVAVVAA', 'VVAAVVVA', 'VVAVAVAA'], 'coarse': 'a', 'small': 'a', 'bb': [10000.0, 10000.0, 0.0],
+    'bf': [10000.0, 10000.0, 2000.0], 'bp': 0.0, 'pv': 0.0, 'pa': 3000.0})
+NUDGE = "82,1,0,2 113,1,0,1 115,1,0,1 117,1,0,1 132,1,0,1 134,1,0,1 177,1,50,0 194,2,20,0 207,1,-50,0 214,20,-50,0 237,1,0,2 240,1,0,2 247,2,-8,0 251,13,-3,0 271,9,3,0 280,3,-47,0 283,1,-47,2 284,1,-50,0 285,1,-50,2 286,1,-50,0 287,1,-50,2 288,1,-50,0 289,1,-70,2 290,6,-70,0 296,1,-120,0 297,3,-70,0 300,3,-20,0 303,1,-20,2 304,1,-20,0 305,1,-20,2 306,3,-20,0 309,1,0,2 334,1,50,0 342,1,20,0 383,1,0,2 385,1,0,2 387,1,0,1 391,1,0,2 393,1,0,2 413,6,8,0 422,1,0,1 433,1,20,0 441,5,-20,0 446,1,-20,2 447,14,-20,0 499,6,-3,0 514,2,20,0 516,1,28,2 517,1,28,0 518,1,28,2 519,15,-22,0 534,2,-42,0 536,3,-50,0 539,6,-20,0 546,6,8,0 560,12,-8,0 572,1,-8,2 573,7,-8,0 582,1,0,2 591,1,-20,0 656,6,-8,0 666,6,-3,0 674,1,-8,0 678,1,-20,2 682,1,-50,2 683,1,-50,0 684,1,-50,2 690,1,0,2 691,1,-50,0 692,1,-50,2 693,4,-50,0 697,3,-42,0 700,1,-42,2 701,1,-42,0 702,1,8,2 703,1,8,0 710,4,8,0 714,2,58,0 716,1,8,0 778,6,-50,0 797,2,8,0 855,1,0,2 869,1,0,2 871,1,0,2 873,1,8,0 874,1,-42,0 875,1,8,2 876,3,8,0 879,1,0,2 880,2,-50,0 884,1,-50,0 887,6,-8,0 896,1,0,2 900,1,0,1 902,1,0,1 906,1,0,2 908,1,0,1 909,7,-3,0 916,1,17,1 917,12,-3,0 1057,5,3,0 1062,15,-17,0 1077,5,-20,0 1100,1,20,0 1105,20,-3,0 1129,1,0,1 1135,1,0,1 1165,2,11,0 1167,4,3,0 1198,6,-3,0 1251,3,-8,0 1254,3,-11,0 1257,3,-3,0"
+CFG["nudge"] = dict((a + j, (c, d)) for a, b, c, d in [map(int, x.split(",")) for x in NUDGE.split()] for j in range(b))
+
+
+def width(a):
+    if a[0] == "ind":
+        return 16 * (a[2][2] - a[2][1])
+    return (a[2] - a[1] + a[3] - 1) // a[3]
+
+
+def dty(a):
+    return SCRATCH[a[1][0] if a[0] == "ind" else a[0]][2]
+
+
+def R(n, a=0, b=None, s=1):
+    return (n, a, SCRATCH[n][1][1] if b is None else b, s)
+
+
+def C(n, j):
+    return (n, j, j + 1, 1)
+
+
+def declare(cfg):
+    ops = []
+
+    def add(eng, kind, args, outs, ins, cost, sem=None, after=None):
+        rd, wr = [], []
+        for a in ins:
+            if isinstance(a, tuple):
+                rd.extend([a[1], a[2]] if a[0] == "ind" else [a])
+        for a in outs:
+            if a[0] == "ind":
+                wr.append(a[1]); rd.append(a[2])
+            else:
+                wr.append(a)
+        ops.append({"eng": eng, "kind": kind, "args": args, "rd": rd, "wr": wr, "cost": cost, "sem": sem,
+                    "after": after, "n": len(args) if kind == "mm" else 1, "alt": None, "bias": bias[0]})
+        return len(ops) - 1
+
+    bias = [0.0]
+
+    def either():
+        b = ops.pop()
+        a = ops[-1]
+        a["alt"] = (b["eng"], b["kind"], b["args"], b["cost"])
+        a["rd"] = a["rd"] + b["rd"]
+
+    def stepf(out, a, c, sign):
+        ts(out, a, float(c), None, AL.is_le if sign < 0 else AL.is_ge)
+        act(out, a, AF.Sigmoid, bias=128.0 - 256.0 * sign * c, scale=256.0 * sign)
+        either()
+
+    def cyc(out, in0, base):
+        n = width(in0)
+        if out[0] == "ind":
+            return cfg["fix"] + cfg["sc"] * n
+        if in0[0] == "ind":
+            return cfg["fix"] + cfg["g"] * n
+        if base == 1 and dty(out) in (H, U) and dty(in0) in (H, U):
+            base = 0.5
+        return cfg["fix"] + max(64, base * n)
+
+    def ts(out, in0, s1, s2, o0, o1=None):
+        add("v", "ts", (out, in0, s1, s2, o0, o1), [out], [in0, s1, s2], cyc(out, in0, 1))
+
+    def tt(out, a, b, op):
+        add("v", "tt", (out, a, b, op), [out], [a, b], cyc(out, a, 1.01 if a[0] in PS or b[0] in PS else 2))
+
+    def cp(out, a):
+        add("v", "cp", (out, a), [out], [a], cyc(out, a, 1))
+
+    def scan(out, a, b, ini, o0, o1):
+        add("v", "scan", (out, a, b, ini, o0, o1), [out], [a, b, ini], cyc(out, a, 1))
+
+    def ms(out, v):
+        add("v", "ms", (out, v), [out], [], cyc(out, out, 1))
+
+    def act(out, a, fn, bias=None, scale=None):
+        add("a", "act", (out, a, fn, bias, scale), [out], [a, bias, scale], cyc(out, a, 1.01))
+
+    def mm(lst):
+        c = sum(max(64, width(m[2])) * (4 if dty(m[2]) == F else 1) for m in lst) * cfg["pe"] + 30
+        add("p", "mm", lst, [m[0] for m in lst], [m[1] for m in lst] + [m[2] for m in lst], c)
+
+    def iota(out, pat, base, cm):
+        add("g", "iota", (out, pat, base, cm), [out], [], 130 + 2 * width(out))
+
+    nd = [0]
+
+    def dma(q, out, a, nbytes):
+        nd[0] += 1
+        add(q, "dma", (out, a), [] if out[0] == "hbm" else [out], [] if a[0] == "hbm" else [a],
+            2000 + 128 * nbytes / 200.0, sem="d%d" % nd[0])
+
+    def move(src, dst, shift, nbytes):
+        nd[0] += 1
+        k = add("g", "rem", (src, dst, shift, "r%d" % nd[0]), [], [src], 2500 + 128 * nbytes / cfg["link"], sem="ls")
+        add("x", "arr", (), [dst], [], 1, sem="r%d" % nd[0], after=k)
+
+    def gather(out, win, off):
+        act(out, ("ind", win, off), AF.Copy)
+        cp(out, ("ind", win, off))
+        either()
+
+    def scale(out, a, s):
+        act(out, a, AF.Identity, scale=s)
+        ts(out, a, s, None, AL.mult)
+        either()
+
+    dma("s", R("pra", 0, 3), ("hbm", "obs", 0, 3), 12)
+    dma("s", C("pra", 3), ("hbm", "eps", 0, 1), 4)
+    dma("s", R("b0s", 0, 1024), ("hbm", "b0", 0, 1024), 2048)
+    dma("a", R("b0s", 1024, 2048), ("hbm", "b0", 1024, 2048), 2048)
+    dma("s", R("f0s", 0, 1024), ("hbm", "f0", 0, 1024), 2048)
+    dma("a", R("f0s", 1024, 2048), ("hbm", "f0", 1024, 2048), 2048)
+    dma("s", R("pis"), ("hbm", "pi", 0, 256), 1024)
+    for j, nm in ((4, "lam"), (5, "rf"), (6, "rb")):
+        dma("s", C("pra", j), ("hbm", nm, 0, 1), 4)
+    dma("s", R("nza"), ("hbm", "nz", 0, S), 4096)
+
+    rc = C("rc", 0)
+    iota(R("iod"), [[1, 144]], 0, -1)
+    iota(C("rci", 0), [[1, 1]], 0, 1)
+    iota(R("j16"), [[0, 17], [1, 16]], 0, 0)
+    iota(R("c16"), [[16, 256]], 0, 0)
+    iota(R("mc"), [[0, 2], [16, 256]], int(MG), 0)
+    iota(R("nb16"), [[-16, 272]], -24, 0)
+    iota(R("tbc"), [[16, 17]], 300, 0)
+    ts(C("rci", 1), C("rci", 0), 15, None, AL.bitwise_and)
+    cp(rc, C("rci", 1))
+    ts(R("q1"), R("iod"), rc, 15.0, AL.add, AL.is_equal)
+    ts(R("ta"), R("iod", 0, 128), rc, 15.0, AL.add, AL.is_le)
+    ts(R("tc"), R("iod", 0, 128), rc, 0.0, AL.add, AL.is_ge)
+    tt(R("bo"), R("ta"), R("tc"), AL.mult)
+    ts(R("tc"), R("iod", 0, 128), 0.0, None, AL.is_ge)
+    tt(R("tri"), R("ta"), R("tc"), AL.mult)
+    ts(R("dmask"), R("j16"), rc, BIG, AL.is_equal, AL.mult)
+    scale(R("bo16"), R("bo"), 16.0)
+    rng = []
+    for b in range(8):
+        p0, p1 = (256 * b + 16) / 2048.0, (b + 1) / 8.0
+        rng.append((0 if b == 0 else int(256 * p0 / (2 - p0)) // 2 * 2, min(256, int(512 * p1 / (1 + p1)) // 2 * 2 + 2)))
+    z0 = [sum(256 - r[0] for r in rng[:b]) - rng[b][0] for b in range(8)]
+    for x in cfg["order"][0]:
+        for b in range(8):
+            if rng[b][1] < 256:
+                iota(R("zc" + x, z0[b] + rng[b][1], z0[b] + 256), [[0, 256 - rng[b][1]]], 1, 0)
+    for x in "fb":
+        iota(C("o" + x, 0), [[0, 1]], 0, 0)
+        iota(R("st" + x, 128, 136), [[0, 8]], int(MG) + 5000, 0)
+    ts(R("idf"), R("iod", 0, 128), 0.0, None, AL.is_equal)
+    scale(R("idb"), R("idf"), 1.0)
+    scale(R("ta"), R("idf"), 63.0)
+    tt(R("str"), R("ta"), R("tri"), AL.add)
+    ts(R("ta"), R("iod", 0, 128), 16.0, None, AL.is_equal)
+    ts(R("tc"), R("iod", 0, 128), -112.0, None, AL.is_equal)
+    tt(R("shf"), R("ta"), R("tc"), AL.add)
+    scale(R("shb"), R("shf"), 1.0)
+    ts(C("rc", 1), rc, -16.0, None, AL.add)
+    scale(R("qw"), R("q1"), C("rc", 1))
+    tt(R("qd", 0, 143), R("qw", 0, 143), R("qw", 1, 144), AL.subtract)
+    ts(C("rci", 0), C("rci", 1), 1, None, AL.bitwise_and)
+    ts(C("rc", 2), C("rci", 0), float(WB - 1 - WF), float(WF), AL.mult, AL.add)
+    tt(C("rc", 3), C("rc", 2), rc, AL.add)
+    ts(R("nfill"), R("c16"), C("rc", 3), -1.0, AL.add, AL.mult)
+    ts(R("tbc"), R("tbc"), rc, None, AL.add)
+    ts(R("eg"), R("iod", 0, 136), 2.0, rc, AL.mult, AL.add)
+    ts(R("ef"), R("eg"), 16.0, -1.0, AL.is_equal, AL.mult)
+    ts(R("eg"), R("eg"), 15.0, -1.0, AL.is_equal, AL.mult)
+    for r, v in ((R("k16"), 16), (R("win", 0, 8), 0), (C("po", 0), 0), (C("nn", 0), -8), (R("nn", 256, 280), -8)):
+        iota(r, [[0, width(r)]], v, 0)
+    cp(R("pia"), R("pis"))
+    move(R("pra", 0, 7), R("prb", 0, 7), -1, 28)
+    move(R("pra", 0, 4), R("prc", 0, 4), 1, 16)
+    move(R("pra", 0, 4), R("prd", 0, 4), -2, 16)
+    move(R("pia"), R("pib"), -1, 512)
+    move(R("nza"), R("nzb"), -1, 4096)
+    for x in "abcd":
+        scale(R("pn" + x, 0, 4), R("pr" + x, 0, 4), -1.0)
+        scale(C("pn" + x, 4), C("pr" + x, 3), -SC)
+
+    def sel(i):
+        return R("q1", 15 - i, 143 - i)
+
+    def ancestors(t, x, pool, par, res):
+        pr, pn = "pr" + par, "pn" + par
+        bank = "ps4" if x == "b" else "ps7"
+        m0 = 0 if x == "b" else S
+        how = cfg["hit"][t][x]
+        cw = S // len(how)
+        for k, h in enumerate(how):
+            a, b = k * cw, (k + 1) * cw
+            src = [R("mw", m0 + a, m0 + b)]
+            if h == "D":
+                ts(src[0], R(pool, a, b), C(pr, t), C(pr, 3), AL.subtract, AL.is_gt)
+                src.append(R("hit", a, b))
+                ts(src[1], R(pool, a, b), C(pr, t), C(pn, 3), AL.subtract, AL.is_lt)
+            else:
+                act(R("aw", a, b), R(pool, a, b), AF.Abs, bias=C(pn, t))
+                act(src[0], R("aw", a, b), AF.Relu, bias=C(pn, 4), scale=SC)
+                ts(src[0], R("aw", a, b), C(pr, 3), None, AL.is_gt)
+                either()
+            lst = [(R(bank, a // 16, b // 16), sel(i), (s[0], s[1] + i, s[2], 16)) for s in src for i in range(16)]
+            mm([m + (j == 0, j == len(lst) - 1) for j, m in enumerate(lst)])
+        w, o, tq = R("w" + x), "o" + x, "tq" + x
+        ts(w, R(bank, 0, 128), 0.0, 1.0, AL.is_le, AL.add)
+        mm([(R(bank, 256, 384), R("bo"), w, True, True), (R(bank, 128, 256), R("tri"), w, True, True)])
+        scan(R(o, 1, 129), R(bank, 256, 384), R("nb16", 0, 128), 0.0, AL.add, AL.max)
+        ts(C(tq, 0), C(o, 128), 1.0 / K, None, AL.mult)
+        scan(R("ec" + x), R("dmask", 0, 128), R(o, 1, 129), 0.0, AL.add, AL.min)
+        if cfg["coarse"] == "a":
+            ts(C(tq, 2), C(o, 128), 16.0, None, AL.mult)
+            ts(R("en" + x), R("ec" + x, 15, 128, 16), -65536.0, 128.0, AL.mult, AL.add)
+        bk2 = "ps5" if x == "b" else "ps6"
+        out = R(bk2, 0, 256)
+        for b in range(8):
+            lo, hi = rng[b]
+            z = R("zc" + x, z0[b] + lo, z0[b] + hi)
+            ts(z, R("c16", lo, hi), C(tq, 0), C("ec" + x, 16 * b + 15), AL.mult, AL.is_ge)
+            if cfg["coarse"] == "a":
+                act(z, R("c16", lo, hi), AF.Sigmoid, bias=C("en" + x, b), scale=C(tq, 2))
+                either()
+            mm([(R(bk2, 256 + lo, 512), R("bo16"), R("zc" + x, z0[b] + lo, z0[b] + 256), b == 0, b == 7)])
+        add("v", "rcp", (C(tq, 1), C(tq, 0)), [C(tq, 1)], [C(tq, 0)], 250)
+        cc = R(bank, 384, 512)
+        tt(cc, R(o, 0, 128), R(bank, 128, 256), AL.add)
+        if cfg["small"] == "a":
+            act(R("qm" + x), cc, AF.Identity, bias=MG, scale=C(tq, 1))
+        else:
+            ts(R("qm" + x), cc, C(tq, 1), MG, AL.mult, AL.add)
+        ts(R("qt" + x), R("qm" + x), -MG, C(tq, 0), AL.add, AL.mult)
+        tt(R(bank, 0, 128), cc, R("qt" + x), AL.is_gt)
+        tt(R("st" + x, 0, 128), R(bank, 0, 128), R("qm" + x), AL.add)
+        scan(R("eb" + x), R("dmask", 0, 256), R(bk2, 256, 512), 0.0, AL.add, AL.min)
+        ts(R("l2" + x, 0, 16), R("eb" + x, 15, 256, 16), 1.0 / 16, None, AL.mult)
+        ts(R("l2" + x, 16, 32), R("eb" + x, 15, 256, 16), 1.0 / 16, 1.0, AL.mult, AL.add)
+        tt(R("x12" + x), ("ind", R("st" + x), R("l2" + x)), R("mc"), AL.subtract)
+        if cfg["q"] == "a":
+            act(R(bank, 0, 256), R("x12" + x, 0, 256), AF.Sigmoid, bias=128.0, scale=-256.0)
+        else:
+            ts(R(bank, 0, 256), R("x12" + x, 0, 256), 0.0, None, AL.is_le)
+        tt(R(bank, 256, 512), R(bank, 0, 256), R("x12" + x, 256, 512), AL.mult)
+        tt(R("xs" + x), R(bank, 256, 512), R("x12" + x, 0, 256), AL.max)
+        act(R("p0" + x), R("x12" + x, 0, 256), AF.Sigmoid, bias=128.0, scale=-256.0)
+        ts(R("p0" + x), R("x12" + x, 0, 256), 0.0, None, AL.is_le)
+        either()
+        mm([(R(bk2, rng[b][0], 256), R("bo16"), R("zc" + x, z0[b] + rng[b][0], z0[b] + 256), b == 0, False) for b in range(8)]
+           + [(out, R("bo"), R("p0" + x), False, False)])
+        for i in range(1, 16):
+            z = R("zz" if x == "b" else "hit", 256 * i, 256 * i + 256)
+            stepf(z, R("xs" + x), i, -1)
+            mm([(out, sel(i), z, False, i == 15)])
+        cp(R(res), out)
+
+    def filling(t, a, b):
+        h = b == 256
+        e = b + 16 * h
+        if t < 2 and cfg["small"] == "a":
+            act(R("ok", a, b), R("ps7", a, b), AF.Sigmoid, bias=7.5 * 256, scale=-256.0)
+        else:
+            ts(R("ok", a, b), R("ps7", a, b), 7.5, None, AL.is_le)
+        ex, cs = R("ps4", a, b), R("ps4", 256 + a, 256 + b)
+        mm([(cs, R("bo"), R("ok", a, b), True, True), (ex, R("str"), R("ok", a, b), True, True)])
+        scan(R("po", a + 1, b + 1), cs, R("nb16", a, b), C("po", a), AL.add, AL.max)
+        if h:
+            ts(R("po", 257, 273), R("k16"), C("po", 256), None, AL.add)
+        cp(R("oi", a, e), R("po", a, e))
+        ts(R("pa", a, e), R("oi", a, e), 15, None, AL.bitwise_and)
+        tt(R("px", a, b), ex, R("pa", a, b), AL.add)
+        ts(R("py", a, b), R("px", a, b), 79, None, AL.bitwise_and)
+        cp(R("pc", a, b), R("py", a, b))
+        v = R("ps6", a, b)
+        for i in range(16):
+            z = R("zz", 256 * i + a, 256 * i + b)
+            if t < 2:
+                stepf(z, R("pc", a, b), 64 + i, 1)
+            else:
+                ts(z, R("pc", a, b), 64.0 + i, None, AL.is_ge)
+            mm([(v, R("qd" if i else "qw", 15 - i, 143 - i), z, i == 0, i == 15)])
+        ts(R("pg", a, e), R("pa", a, e), rc, BIG, AL.is_le, AL.mult)
+        w = e - a
+        for k in range(2):
+            scan(R("pe", 2 * a + k * w, 2 * a + k * w + w), R("dmask", a, e), R("po", a + k, e + k), 0.0, AL.add, AL.min)
+        k0, k1, k2 = a // 8, a // 8 + w // 16, a // 8 + w // 8
+        ts(R("pk2", k0, k2), R("pe", 2 * a + 15, 2 * e, 16), 1.0 / 16, -15.0 / 32, AL.mult, AL.add)
+        q, q2 = R("pq", a // 16, e // 16), R("pq2", a // 16, e // 16)
+        tt(q, R("pk2", k0, k1), R("pk2", k1, k2), AL.is_equal)
+        tt(q2, q, R("tbc", a // 16, e // 16), AL.mult)
+        tt(q, q2, R("pk2", k0, k1), AL.add)
+        cp(R("pl", a // 16, e // 16), q)
+        if cfg["small"] == "a":
+            act(R("d0", a, b), v, AF.Identity, scale=BIG)
+        else:
+            ts(R("d0", a, b), v, BIG, None, AL.mult)
+        tt(R("t1", a, b), R("nb16", a, b), v, AL.subtract)
+        scan(R("nn", a + 1, b + 1), R("d0", a, b), R("t1", a, b), C("nn", a), AL.add, AL.max)
+        if h:
+            ts(C("nn", 257), C("pa", 256), C("po", 256), C("rc", 3), AL.subtract, AL.subtract)
+        tt(R("yy", a, e), R("nn", a, e), R("pg", a, e), AL.subtract)
+        tt(("ind", R("pw"), R("pl", a // 16, e // 16)), R("nn", a + 1, e + 1), R("yy", a, e), AL.max)
+
+    pools = [{"f": "f0s", "b": "b0s"}, {"f": "fp1", "b": "lb"}, {"f": "lf", "b": "lb"}]
+    dest = [{"f": "fp1", "b": "sb0"}, {"f": "sf1", "b": "lb"}, {"f": "fp1", "b": "lb"}]
+    for t in range(3):
+        par = "b" if t == 1 else "a"
+        pr, pn = "pr" + par, "pn" + par
+        bias[0] = 0.0
+        dma("s", R("pw", 0, 256), R("nfill"), 1024)
+        al = {"f": "laf" if t == 2 else "alf", "b": "lab" if t == 1 else "alb"}
+        for x in cfg["order"][t]:
+            bias[0] = cfg["bb"][t] if x == "b" else cfg["bf"][t]
+            if al[x][0] == "a":
+                ancestors(t, x, pools[t][x], par, al[x])
+            else:
+                ancestors(t, x, dest[t - 1][x], "c" if t == 1 else "d", "sa" + x)
+                move(R("sa" + x), R(al[x]), -2 if t == 1 else 2, 512)
+        bias[0] = 0.0
+        cw = K // cfg["bA"]
+        for k in range(cfg["bA"]):
+            gather(R("win", WB + k * cw, WB + (k + 1) * cw), R(pools[t]["b"]), R(al["b"], k * cw // 16, (k + 1) * cw // 16))
+        a = 0
+        for k, cw in enumerate(cfg["gch"]):
+            b = a + cw
+            fi, d, m = R("win", WF + a, WF + b), R("dd", a, b), R("win", WM + a, WM + b)
+            e = R("psa" if k % 2 == 0 else "psb", 0, cw)
+            gather(fi, R(pools[t]["f"]), R(al["f"], a // 16, b // 16))
+            tt(d, ("ind", R("win", WB, WW), R("pi" + par, a // 16, b // 16)), fi, AL.subtract)
+            act(e, d, AF.Identity, scale=C(pr, 4))
+            tt(m, fi, e, AL.add)
+            act(R("ab", a, b), m, AF.Abs, bias=C(pn, t))
+            if cfg["acc"][t][k] == "V":
+                ts(R("hit", a, b), R("ab", a, b), C(pr, 3), None, AL.is_gt)
+            else:
+                act(R("hit", a, b), R("ab", a, b), AF.Relu, bias=C(pn, 4), scale=SC)
+                act(R("hit", a, b), R("hit", a, b), AF.Sign)
+                ts(R("hit", a, b), R("hit", a, b), 0.0, None, AL.is_gt)
+                either()
+            mm([(R("ps7", a // 16, b // 16), sel(i), R("hit", a + i, b, 16), i == 0, i == 15) for i in range(16)])
+            if t == 2:
+                act(R("tb", a, b), d, AF.Square)
+                act(R("tb", a, b), R("tb", a, b), AF.Exp, scale=-1.0)
+                for z in range(a, b, 256):
+                    mm([(R("ps5", 0, 256), R("idf"), R("tb", z, z + 256), z == 0, z == K - 256)])
+            if b // 16 in cfg["parts"]:
+                j = cfg["parts"].index(b // 16)
+                bias[0] = cfg["bp"]
+                filling(t, cfg["parts"][j - 1] if j else 0, b // 16)
+                bias[0] = 0.0
+            a = b
+        if t == 2:
+            act(R("yes"), R("ps5", 0, 256), AF.Copy)
+            dma("s", ("hbm", "ye", 0, 256), R("yes"), 1024)
+        seq = cfg["step"][t]
+        for x in (seq[0], "f" if seq[0] == "b" else "b"):
+            j = 0 if x == "f" else 1
+            u, mat = R("ps7" if j else "ps4", 0, 128), "eg" if j else "ef"
+            mm([(u, R(mat, 8, 136), R("pw", 0, 256, 2), True, False), (u, R(mat, 0, 128), R("pw", 1, 256, 2), False, True)])
+            cp(R("ll", 128 * j, 128 * j + 128), u)
+        pos = {"f": 0, "b": 0}
+        for k, x in enumerate(seq):
+            j = 0 if x == "f" else 1
+            bias[0] = cfg["s" + x][t]
+            sa = sum(cfg["sch"][t][:pos[x]])
+            cw = cfg["sch"][t][pos[x]]
+            sb = sa + cw
+            pos[x] += 1
+            a, b = j * S + sa, j * S + sb
+            src = ("ind", R("win"), R("ll", a // 16, b // 16))
+            act(R("ab", a, b), src, AF.Square)
+            tt(R("dd", a, b), src, R("ab", a, b), AL.subtract)
+            u = R("psa" if k % 4 < 2 else "psb", 512 * (k % 2), 512 * (k % 2) + cw)
+            mat = "sh" if x == "b" and t < 2 else "id"
+            if mat == "sh" or cfg["nzp"][t][k] == "P":
+                scale(R("tb", a, b), R("dd", a, b), C(pr, 5 + j))
+                mm([(u, R(mat + "f"), R("tb", a, b), True, False), (u, R(mat + "b"), R("nz" + par, sa, sb), False, True)])
+            else:
+                act(u, R("dd", a, b), AF.Identity, scale=C(pr, 5 + j))
+                tt(R("tb", a, b), u, R("nz" + par, sa, sb), AL.add)
+                u = R("tb", a, b)
+            new = R(dest[t][x], sa, sb)
+            ts(new, u, 0.0, 1.0, AL.max, AL.min)
+            if t == 2:
+                dma("s", ("hbm", "y" + x, sa, sb), new, 4 * cw)
+            elif t == 0 and x == "b":
+                move(new, R("lb", sa, sb), -2, 4 * cw)
+            elif t == 1 and x == "f":
+                move(new, R("lf", sa, sb), 2, 4 * cw)
+    return ops
+
+
+def banks(a):
+    return range(PS[a[0]][1] + a[1] // 512, PS[a[0]][1] + (a[2] - 1) // 512 + 1)
+
+
+def prepare(cfg):
+    ops = declare(cfg)
+    n = len(ops)
+    acc = {}
+    last = {}
+    for i, o in enumerate(ops):
+        dep = set() if o["after"] is None else {o["after"]}
+        for lst, wr in ((o["rd"], False), (o["wr"], True)):
+            for a in lst:
+                for (j, c0, c1, w) in acc.get(a[0], []):
+                    if (w or wr) and c0 < a[2] and a[1] < c1:
+                        dep.add(j)
+        bk = set(b for a in o["rd"] + o["wr"] if a[0] in PS for b in banks(a))
+        for b in bk:
+            prev, cur = last.get(b, ([], []))
+            if cur and ops[cur[-1]]["eng"] != o["eng"]:
+                prev, cur = cur, []
+            dep.update(prev)
+            if cur and o["eng"] == "p":
+                dep.add(cur[-1])
+            last[b] = (prev, cur + [i])
+        for lst, wr in ((o["rd"], False), (o["wr"], True)):
+            for a in lst:
+                if wr:
+                    acc[a[0]] = [e for e in acc.get(a[0], []) if not (a[3] == 1 and a[1] <= e[1] and e[2] <= a[2])]
+                acc.setdefault(a[0], []).append((i, a[1], a[2], wr))
+        dep.discard(i)
+        o["dep"] = dep
+    succ = [[] for _ in range(n)]
+    for i, o in enumerate(ops):
+        for j in o["dep"]:
+            succ[j].append(i)
+    pri = [0.0] * n
+    for i in range(n - 1, -1, -1):
+        pri[i] = ops[i]["cost"] + max([pri[j] + cfg["lat"] for j in succ[i]], default=0.0)
+    rs = np.random.RandomState(cfg["seed"])
+    pri = [p + o["bias"] + cfg["noise"] * float(x) for p, o, x in zip(pri, ops, rs.rand(n))]
+    return ops, succ, pri
+
+
+def schedule(cfg, ops, succ, pri, nudge):
+    n = len(ops)
+    free = dict((e, 0.0) for e in "vapgsx")
+    link = 0.0
+    done, start, took = [0.0] * n, [0.0] * n, [False] * n
+    left = [len(o["dep"]) for o in ops]
+    at = [0.0] * n
+    ready = dict((e, {}) for e in "vapgsx")
+
+    def offer(i):
+        o = ops[i]
+        d, f = nudge.get(i, (0, 0))
+        if f != 2 or not o["alt"]:
+            ready[o["eng"]][i] = pri[i] + 100.0 * d
+        if f != 1 and o["alt"]:
+            ready[o["alt"][0]][i] = pri[i] + 100.0 * d - cfg["p" + o["alt"][0]]
+
+    for i in range(n):
+        if left[i] == 0:
+            offer(i)
+    order = []
+    while len(order) < n:
+        best = None
+        for e in "vapgsx":
+            c = ready[e]
+            if c:
+                t0 = max(free[e], min(at[i] for i in c))
+                if best is None or t0 <= best[0][0]:
+                    i = max((c[i], -i) for i in c if at[i] <= t0 + 1)[1]
+                    key = (t0, ops[-i]["eng"] != e)
+                    if best is None or key < best[0]:
+                        best = (key, -i, e)
+        (t0, alt), i, e = best
+        o = ops[i]
+        took[i] = alt
+        ready[o["eng"]].pop(i, None)
+        if o["alt"]:
+            ready[o["alt"][0]].pop(i, None)
+        if o["kind"] == "dma":
+            free[e] = t0 + 60; done[i] = t0 + o["cost"]
+        elif o["kind"] == "rem":
+            free[e] = t0 + 500
+            done[i] = link = max(link, t0 + 2500) + o["cost"] - 2500
+        else:
+            done[i] = free[e] = t0 + (o["alt"][3] if alt else o["cost"])
+        start[i] = t0
+        order.append(i)
+        for j in succ[i]:
+            left[j] -= 1
+            at[j] = max(at[j], done[i] + (0 if e == "p" == ops[j]["eng"] else cfg["lat"]))
+            if left[j] == 0:
+                offer(j)
+    return order, took, start, done
+
+
+def plan(cfg):
+    ops, succ, pri = prepare(cfg)
+    order, took, start, done = schedule(cfg, ops, succ, pri, cfg["nudge"])
+    for i, o in enumerate(ops):
+        o["took"], o["t0"], o["t1"] = took[i], start[i], done[i]
+        if took[i]:
+            o["eng"], o["kind"], o["args"], o["cost"] = o["alt"]
+    count = dict((e, 0) for e in "vapg")
+    known = dict((e, {}) for e in "vapgsx")
+    for i in order:
+        o = ops[i]
+        kn = known[o["eng"]]
+        o["wait"] = []
+        need = {}
+        for j in o["dep"]:
+            p = ops[j]
+            if o["eng"] == "x" or (p["eng"] == "p" and o["eng"] == "p"):
+                continue
+            if kn.get(p["tag"][0], 0) < p["tag"][1] and need.get(p["tag"][0], (0,))[0] < p["tag"][1]:
+                need[p["tag"][0]] = (p["tag"][1], j)
+        for s in sorted(need, key=lambda s: -done[need[s][1]]):
+            val, j = need[s]
+            if kn.get(s, 0) >= val:
+                continue
+            o["wait"].append((s, val))
+            for s2, v2 in ops[j]["clock"].items():
+                kn[s2] = max(kn.get(s2, 0), v2)
+        o["inc"] = False
+        if o["kind"] == "dma":
+            o["tag"] = (o["sem"], 16)
+        elif o["kind"] in ("arr", "rem"):
+            o["tag"] = (o["sem"], 1)
+        else:
+            o["inc"] = bool(succ[i])
+            if o["inc"]:
+                count[o["eng"]] += o["n"]
+            o["tag"] = ("c" + o["eng"], count[o["eng"]])
+        o["clock"] = {} if o["eng"] == "x" else dict(kn)
+        o["clock"][o["tag"][0]] = o["tag"][1]
+    return ops, order, count
+
+
+OPS, ORDER, COUNT = plan(CFG)
+SEMAPHORES = ["cv", "ca", "cp", "cg", "ls"] + [o["sem"] for o in OPS if o["kind"] in ("dma", "arr")]
+
+
+def rank_program(g, core, T, topo):
+    rank = T.rank_of(core)
+    if rank is None:
+        return
+    q = {"v": g.vector, "a": g.scalar, "p": g.tensor, "g": g, "s": g.sync}
+
+    def ap(a):
+        if not isinstance(a, tuple):
+            return a
+        if a[0] == "ind":
+            return ap(a[1]).indirect(ap(a[2]))
+        if a[0] == "hbm":
+            return T[a[1]][:] if a[3] - a[2] == T[a[1]].shape[1] else T[a[1]][:, a[2]:a[3]]
+        return T[a[0]][:, a[1]:a[2]] if a[3] == 1 else T[a[0]][:, a[1]:a[2]:a[3]]
+
+    arrive = {}
+    for o in OPS:
+        if o["kind"] == "rem":
+            arrive[o["args"][3]] = len(topo.engines(T.cores[(rank - o["args"][2]) % N], core))
+    sent = 0
+    for i in ORDER:
+        o = OPS[i]
+        if o["eng"] == "x":
+            continue
+        e, k, a = q[o["eng"]], o["kind"], o["args"]
+        for s, val in o["wait"]:
+            e.wait_ge(T.sem[s], arrive.get(s, val))
+        if k == "rem":
+            dst = T.cores[(rank + a[2]) % N]
+            rid, pid, _ = topo.addr(dst)
+            g.remote_dma(ap(a[1]), ap(a[0]), T.sem[a[3]], T.sem.ls, pid, rid, topo.mask(core, dst))
+            sent += len(topo.engines(core, dst))
+            continue
+        if k == "dma":
+            e.dma_start(ap(a[0]), ap(a[1])).then_inc(T.sem[o["sem"]], 16)
+            continue
+        if k == "mm":
+            ins = [e.matmul(ap(m[0]), ap(m[1]), ap(m[2]), m[3], m[4]) for m in a]
+        elif k == "ts":
+            ins = [e.tensor_scalar(*[ap(x) for x in (a if a[5] is not None else a[:5])])]
+        elif k == "tt":
+            ins = [e.tensor_tensor(ap(a[0]), ap(a[1]), ap(a[2]), a[3])]
+        elif k == "cp":
+            ins = [e.tensor_copy(ap(a[0]), ap(a[1]))]
+        elif k == "scan":
+            ins = [e.tensor_tensor_scan(*[ap(x) for x in a])]
+        elif k == "ms":
+            ins = [e.memset(ap(a[0]), a[1])]
+        elif k == "rcp":
+            ins = [e.reciprocal(ap(a[0]), ap(a[1]))]
+        elif k == "iota":
+            if dty(a[0]) == I:
+                ins = [e.iota(ap(a[0]), a[1], a[2], a[3])]
+            else:
+                ins = [e.iota(ap(a[0]), a[1], a[2], a[3], allow_small_or_imprecise_dtypes=True)]
+        else:
+            kw = {}
+            if a[3] is not None:
+                kw["bias"] = ap(a[3])
+            if a[4] is not None:
+                kw["scale"] = ap(a[4])
+            ins = [e.activation(ap(a[0]), ap(a[1]), a[2], **kw)]
+        if o["inc"]:
+            for x in ins:
+                x.then_inc(T.sem["c" + o["eng"]], 1)
+    for x in "vapg":
+        g.wait_ge(T.sem["c" + x], COUNT[x])
+    g.wait_ge(T.sem.ls, sent)
+    for o in OPS:
+        if o["kind"] == "dma":
+            g.wait_ge(T.sem[o["sem"]], 16)
+        elif o["kind"] == "arr":
+            g.wait_ge(T.sem[o["sem"]], arrive[o["sem"]])

@@ -1,14 +1,16 @@
-import numpy as np
-from concourse.bass import DstId, RemoteDMATransfer
-from concourse.mybir import dt, AluOpType, AxisListType, ActivationFunctionType
+import math
+from concourse.mybir import AluOpType, ActivationFunctionType
 
 AL = AluOpType
 AF = ActivationFunctionType
 S, K, N = 2048, 4096, 8
 MG = 12582912.0
-BIG = 32768.0
+M16 = 16 * MG
+BIG = 2.0 ** 26
+PB = 8192.0
 SC = 2.0 ** 60
-WM, WF, WB, WW = 8, 8 + K, 8 + 2 * K, 8 + 3 * K
+LN2 = math.log(2.0)
+WM, WF, WB, WW = 16, 16 + K, 16 + 2 * K, 16 + 3 * K
 
 F, H, I, U = "float32", "bfloat16", "int32", "uint16"
 SCRATCH = {}
@@ -16,49 +18,51 @@ for _n, _w, _d in [
     ("f0s", S, H), ("b0s", S, H), ("nza", S, H), ("nzb", S, H), ("pis", 256, I), ("pia", 256, U), ("pib", 256, U),
     ("pra", 8, F), ("prb", 8, F), ("pna", 8, F), ("pnb", 8, F), ("prc", 8, F), ("prd", 8, F), ("pnc", 8, F), ("pnd", 8, F),
     ("sab", 256, U), ("saf", 256, U), ("lab", 256, U), ("laf", 256, U),
-    ("win", WW, F), ("dd", K, F), ("ab", K, F), ("tb", K, F), ("hit", K, H), ("aw", S, F), ("mw", 2 * S, H),
+    ("win", WW, F), ("dd", K, F), ("ab", K, F), ("tb", K, F), ("hit", K, H), ("mw", 2 * S, H),
     ("fp1", S, F), ("sb0", S, F), ("lb", S, F), ("sf1", S, F), ("lf", S, F), ("yes", 256, F),
-    ("zz", K, H), ("zcf", 1408, H), ("zcb", 1408, H), ("ef", 136, F), ("eg", 136, F),
-    ("iod", 144, F), ("rci", 2, I), ("rc", 4, F), ("j16", 272, F), ("dmask", 272, F), ("c16", 256, H), ("mc", 512, F),
-    ("nb16", 272, F), ("nfill", 256, F), ("tbc", 17, I), ("k16", 16, F), ("ta", 128, F), ("tc", 128, F),
-    ("q1", 144, H), ("qw", 144, H), ("qd", 144, H), ("bo", 128, H), ("bo16", 128, H), ("tri", 128, H), ("str", 128, H),
-    ("idb", 128, H), ("shb", 128, H), ("idf", 128, F), ("shf", 128, F),
-    ("ok", 256, H), ("po", 280, F), ("oi", 272, I), ("pa", 272, I), ("pg", 272, F), ("px", 256, I), ("py", 256, I),
-    ("pc", 256, H), ("pe", 544, F), ("pk", 34, I), ("pk2", 34, I), ("pq", 17, I), ("pq2", 17, I), ("pl", 18, U),
-    ("d0", 256, F), ("t1", 256, F), ("nn", 280, F), ("yy", 272, F), ("pw", 832, F), ("ll", 256, U),
+    ("zcf", 768, H), ("zcb", 768, H), ("cz", 256, H), ("ef", 136, F), ("eg", 136, F),
+    ("iod", 144, F), ("rci", 8, I), ("rc", 12, F), ("j16", 416, F), ("dmask", 416, F), ("c16", 256, H), ("mc", 256, F),
+    ("nc16", 272, H), ("ones", 512, H), ("nfill", 256, F), ("tbc", 17, F),
+    ("q1", 144, H), ("mh", 128 * 22, H), ("mf", 128 * 9, F),
+    ("ok", 272, H), ("po", 280, F), ("f16", 288, H), ("ee", 256, H), ("ff", 1280, F), ("pe", 544, F), ("pq", 18, F),
+    ("pq2", 18, F), ("pl", 18, U), ("nn", 280, F), ("yy", 272, F), ("pw", 576, F), ("ll", 256, U),
 ]:
     SCRATCH[_n] = ("sbuf", [128, _w], _d)
 for _x in "fb":
-    for _n, _w, _d in [("w", 128, H), ("o", 136, F), ("tq", 4, F), ("en", 8, F), ("qm", 128, F), ("qt", 128, F), ("st", 136, F),
-                       ("ec", 128, F), ("eb", 256, F), ("l2", 32, U), ("x12", 512, H), ("p0", 256, H),
-                       ("xs", 256, H), ("al", 256, U)]:
+    for _n, _w, _d in [("w", 128, H), ("o", 136, F), ("tq", 4, F), ("en", 8, F), ("qm", 128, F), ("qt", 128, F), ("st", 1040, F),
+                       ("ec", 128, F), ("eb", 256, F), ("l2", 16, U), ("x12", 512, H), ("xc", 512, H), ("xe", 512, H),
+                       ("p0", 256, H), ("xf", 256, F), ("al", 256, U)]:
         SCRATCH[_n + _x] = ("sbuf", [128, _w], _d)
 PS = {"psa": (1024, 0), "psb": (1024, 2), "ps4": (512, 4), "ps5": (512, 5), "ps6": (512, 6), "ps7": (512, 7)}
 for _n in PS:
     SCRATCH[_n] = ("psum", [128, PS[_n][0]], F)
+MH = ["bo", "bo16", "bo512", "tri", "trk", "str", "stt", "idb", "nid", "shb", "w1", "nw1", "wb0", "wb1", "wb2", "wb3",
+      "dl", "b0", "nb0", "bk", "boh", "bo8"]
+MF = ["idf", "idk", "shf", "gg", "pb0", "pb1", "pb2", "pb3", "pb4"]
 
 CFG = {
-    "gch": [1024, 1024, 1024, 512, 512],
-    "parts": [128, 256],
-    "sch": [[512] * 4, [512] * 4, [512, 512, 512, 256, 256]],
-    "step": ["bbbbffff", "ffffbbbb", "fbfbfbfbfb"], "sf": [0.0, 0.0, 0.0], "sb": [0.0, 0.0, 0.0], "q": "a",
-    "nzp": ["P" * 10, "P" * 10, "P" * 10],
-    "hit": {0: {"b": "AA", "f": "AA"}, 1: {"f": "AAAA", "b": "AAAA"}, 2: {"b": "AAAA", "f": "AAAA"}},
+    "gch": [[512, 1024, 1024, 512, 512, 512]] * 3,
+    "parts": [[96, 192, 256]] * 3,
+    "sch": [[512, 512, 1024], [512, 512, 1024], [1024, 512, 512]],
+    "step": ["bbbfff", "fffbbb", "bfbfbf"],
+    "hit": [{"b": "DD", "f": "AA"}, {"f": "AA", "b": "AA"}, {"b": "AA", "f": "AA"}],
     "order": ["bf", "bf", "fb"],
-    "bA": 4, "acc": ["AAAVV", "AAAVV", "VVVVV"], "coarse": "a", "small": "a",
-    "bb": [0.0, 0.0, 0.0], "bf": [0.0, 0.0, 0.0], "bp": 0.0,
-    "pv": 3000.0, "pa": 3000.0, "noise": 0.0, "seed": 0,
-    "g": 1.56, "sc": 3.8, "pe": 0.5, "lat": 100.0, "fix": 60.0, "link": 60.0, "nudge": {},
+    "bA": ["AVAV"] * 3, "fi": ["AAAAAAAA"] * 3, "acc": ["VVVVVVVV"] * 3, "qm": "A", "p0": "V",
+    "ba": [0.0, 0.0, 0.0], "ye": 0.0, "wait": 300.0, "gap": 500.0, "slope": 1.0, "slope2": 1.0, "passes": 3,
+    "sf": [0.0, 0.0, 0.0], "sb": [0.0, 0.0, 0.0], "bb": [0.0, 0.0, 0.0], "bf": [0.0, 0.0, 0.0], "bp": [3000.0, 0.0, 0.0, 0.0],
+    "pv": 0.0, "pa": 3000.0,
+    "way": ["DRDSD", "DRDSD"], "zc": "VAVAVAVA",
+    "g": 1.56, "sc": 3.8, "pe": 0.55, "lat": 160.0, "fix": 60.0, "link": 50.0, "hop": 100.0,
 }
 CFG.update({
-    'gch': [512] * 8, 'parts': [128, 256], 'sch': [[256, 512, 512, 512, 256], [512, 512, 512, 512], [512, 512, 512, 256, 256]],
-    'step': ['bfbbffbfbf', 'fbbfbbff', 'bbbfffffbb'], 'sf': [-2000.0, 2000.0, 0.0], 'sb': [-2000.0, 2000.0, 0.0], 'q': 'a',
-    'nzp': ['PPPPPPPPVP', 'PPPPPPVPPP', 'PPPPPVPPPP'],
-    'hit': {0: {'b': 'AD', 'f': 'AD'}, 1: {'f': 'AAAA', 'b': 'AA'}, 2: {'b': 'AA', 'f': 'AA'}}, 'order': ['bf', 'bf', 'fb'],
-    'bA': 2, 'acc': ['VVVAVVAA', 'VVAAVVVA', 'VVAVAVAA'], 'coarse': 'a', 'small': 'a', 'bb': [10000.0, 10000.0, 0.0],
-    'bf': [10000.0, 10000.0, 2000.0], 'bp': 0.0, 'pv': 0.0, 'pa': 3000.0})
-NUDGE = "82,1,0,2 113,1,0,1 115,1,0,1 117,1,0,1 132,1,0,1 134,1,0,1 177,1,50,0 194,2,20,0 207,1,-50,0 214,20,-50,0 237,1,0,2 240,1,0,2 247,2,-8,0 251,13,-3,0 271,9,3,0 280,3,-47,0 283,1,-47,2 284,1,-50,0 285,1,-50,2 286,1,-50,0 287,1,-50,2 288,1,-50,0 289,1,-70,2 290,6,-70,0 296,1,-120,0 297,3,-70,0 300,3,-20,0 303,1,-20,2 304,1,-20,0 305,1,-20,2 306,3,-20,0 309,1,0,2 334,1,50,0 342,1,20,0 383,1,0,2 385,1,0,2 387,1,0,1 391,1,0,2 393,1,0,2 413,6,8,0 422,1,0,1 433,1,20,0 441,5,-20,0 446,1,-20,2 447,14,-20,0 499,6,-3,0 514,2,20,0 516,1,28,2 517,1,28,0 518,1,28,2 519,15,-22,0 534,2,-42,0 536,3,-50,0 539,6,-20,0 546,6,8,0 560,12,-8,0 572,1,-8,2 573,7,-8,0 582,1,0,2 591,1,-20,0 656,6,-8,0 666,6,-3,0 674,1,-8,0 678,1,-20,2 682,1,-50,2 683,1,-50,0 684,1,-50,2 690,1,0,2 691,1,-50,0 692,1,-50,2 693,4,-50,0 697,3,-42,0 700,1,-42,2 701,1,-42,0 702,1,8,2 703,1,8,0 710,4,8,0 714,2,58,0 716,1,8,0 778,6,-50,0 797,2,8,0 855,1,0,2 869,1,0,2 871,1,0,2 873,1,8,0 874,1,-42,0 875,1,8,2 876,3,8,0 879,1,0,2 880,2,-50,0 884,1,-50,0 887,6,-8,0 896,1,0,2 900,1,0,1 902,1,0,1 906,1,0,2 908,1,0,1 909,7,-3,0 916,1,17,1 917,12,-3,0 1057,5,3,0 1062,15,-17,0 1077,5,-20,0 1100,1,20,0 1105,20,-3,0 1129,1,0,1 1135,1,0,1 1165,2,11,0 1167,4,3,0 1198,6,-3,0 1251,3,-8,0 1254,3,-11,0 1257,3,-3,0"
-CFG["nudge"] = dict((a + j, (c, d)) for a, b, c, d in [map(int, x.split(",")) for x in NUDGE.split()] for j in range(b))
+    'gch': [[512, 512, 1024, 1024, 512, 512], [512, 1024, 1024, 512, 512, 512], [512, 1024, 1024, 512, 512, 512]],
+    'parts': [[64, 192, 256], [96, 192, 256], [96, 192, 256]],
+    'sch': [[512, 512, 512, 512], [256, 768, 512, 512], [512, 512, 512, 256, 256]], 'step': ['bfbfbfbf', 'fbffbfbb', 'bbbbbfffff'],
+    'hit': [{'b': 'AV', 'f': 'DD'}, {'f': 'AA', 'b': 'VV'}, {'b': 'AA', 'f': 'VV'}], 'order': ['fb', 'fb', 'bf'],
+    'bA': ['AVAV', 'AVAV', 'AVAV'], 'fi': ['AVAAAVVA', 'VAAAAAAV', 'VAVAAAVA'], 'acc': ['VVBVVVVB', 'BVVAVVVV', 'VVVAVVVA'],
+    'qm': 'A', 'p0': 'V', 'ba': [-6000.0, -3000.0, 0.0], 'ye': -10000.0, 'wait': 300.0, 'gap': 2000.0, 'slope': 0.5,
+    'slope2': 0.5, 'passes': 1, 'sf': [500.0, -1500.0, 500.0], 'sb': [500.0, 0.0, 1500.0], 'bb': [-1500.0, 1500.0, 0.0],
+    'bf': [-3000.0, 0.0, -1500.0], 'bp': [3000.0, 6000.0, 6000.0, 0.0], 'pv': 5000.0, 'way': ['DSRSD', 'SDDRS'], 'zc': 'AVAVAVAV'})
 
 
 def width(a):
@@ -72,6 +76,9 @@ def dty(a):
 
 
 def R(n, a=0, b=None, s=1):
+    if n in MH or n in MF:
+        j = 128 * (MH.index(n) if n in MH else MF.index(n))
+        return ("mh" if n in MH else "mf", j, j + 128, 1)
     return (n, a, SCRATCH[n][1][1] if b is None else b, s)
 
 
@@ -98,16 +105,14 @@ def declare(cfg):
 
     bias = [0.0]
 
-    def either():
+    def either(on="?"):
         b = ops.pop()
         a = ops[-1]
-        a["alt"] = (b["eng"], b["kind"], b["args"], b["cost"])
-        a["rd"] = a["rd"] + b["rd"]
-
-    def stepf(out, a, c, sign):
-        ts(out, a, float(c), None, AL.is_le if sign < 0 else AL.is_ge)
-        act(out, a, AF.Sigmoid, bias=128.0 - 256.0 * sign * c, scale=256.0 * sign)
-        either()
+        if on == "?":
+            a["alt"] = (b["eng"], b["kind"], b["args"], b["cost"])
+            a["rd"] = a["rd"] + b["rd"]
+        elif on.lower() == b["eng"]:
+            ops[-1] = b
 
     def cyc(out, in0, base):
         n = width(in0)
@@ -129,7 +134,7 @@ def declare(cfg):
         add("v", "cp", (out, a), [out], [a], cyc(out, a, 1))
 
     def scan(out, a, b, ini, o0, o1):
-        add("v", "scan", (out, a, b, ini, o0, o1), [out], [a, b, ini], cyc(out, a, 1))
+        add("v", "scan", (out, a, b, ini, o0, o1), [out], [a, b, ini], cyc(out, a, 1.01))
 
     def ms(out, v):
         add("v", "ms", (out, v), [out], [], cyc(out, out, 1))
@@ -141,8 +146,14 @@ def declare(cfg):
         c = sum(max(64, width(m[2])) * (4 if dty(m[2]) == F else 1) for m in lst) * cfg["pe"] + 30
         add("p", "mm", lst, [m[0] for m in lst], [m[1] for m in lst] + [m[2] for m in lst], c)
 
+    def group(lst):
+        mm([m + (j == 0, j == len(lst) - 1) for j, m in enumerate(lst)])
+
     def iota(out, pat, base, cm):
-        add("g", "iota", (out, pat, base, cm), [out], [], 130 + 2 * width(out))
+        add("g", "iota", (out, pat, base, cm), [out], [], 160 + 2 * width(out))
+
+    def keep(out, a, pat, op, fill, base, cm):
+        add("g", "sel", (out, a, pat, op, fill, base, cm), [out], [a], 205 + 2 * width(out))
 
     nd = [0]
 
@@ -151,20 +162,25 @@ def declare(cfg):
         add(q, "dma", (out, a), [] if out[0] == "hbm" else [out], [] if a[0] == "hbm" else [a],
             2000 + 128 * nbytes / 200.0, sem="d%d" % nd[0])
 
-    def move(src, dst, shift, nbytes):
+    def move(src, dst, shift, nbytes, via=False):
         nd[0] += 1
-        k = add("g", "rem", (src, dst, shift, "r%d" % nd[0]), [], [src], 2500 + 128 * nbytes / cfg["link"], sem="ls")
+        k = add("g", "rem", (src, dst, shift, "r%d" % nd[0], via), [], [src], 128 * nbytes / cfg["link"], sem="ls")
+        ops[k]["pre"] = 2500 + via * (2500 + 128 * nbytes / cfg["hop"])
+        ops[k]["cost"] += ops[k]["pre"]
         add("x", "arr", (), [dst], [], 1, sem="r%d" % nd[0], after=k)
 
-    def gather(out, win, off):
+    def gather(out, win, off, on):
         act(out, ("ind", win, off), AF.Copy)
         cp(out, ("ind", win, off))
-        either()
+        either(on)
 
-    def scale(out, a, s):
+    def scale(out, a, s, on="?"):
         act(out, a, AF.Identity, scale=s)
         ts(out, a, s, None, AL.mult)
-        either()
+        either(on)
+
+    def reach(p):
+        return min(S, (K * p // (K + p) + 2 + 15) // 16 * 16)
 
     dma("s", R("pra", 0, 3), ("hbm", "obs", 0, 3), 12)
     dma("s", C("pra", 3), ("hbm", "eps", 0, 1), 4)
@@ -178,55 +194,93 @@ def declare(cfg):
     dma("s", R("nza"), ("hbm", "nz", 0, S), 4096)
 
     rc = C("rc", 0)
+    io = R("iod", 0, 128)
     iota(R("iod"), [[1, 144]], 0, -1)
     iota(C("rci", 0), [[1, 1]], 0, 1)
-    iota(R("j16"), [[0, 17], [1, 16]], 0, 0)
+    iota(R("j16"), [[0, 26], [1, 16]], 0, 0)
     iota(R("c16"), [[16, 256]], 0, 0)
-    iota(R("mc"), [[0, 2], [16, 256]], int(MG), 0)
-    iota(R("nb16"), [[-16, 272]], -24, 0)
-    iota(R("tbc"), [[16, 17]], 300, 0)
+    iota(R("nc16"), [[-16, 272]], -16, 0)
+    iota(R("mc"), [[16, 256]], int(MG), 0)
+    iota(R("ones", 0, 128), [[0, 128]], 1, 0)
+    act(R("ones", 128, 512), R("j16", 0, 384), AF.Identity, bias=1.0, scale=0.0)
+    iota(R("tbc"), [[16, 17]], 300 - 1024, 0)
     ts(C("rci", 1), C("rci", 0), 15, None, AL.bitwise_and)
     cp(rc, C("rci", 1))
+    one = R("ones", 0, 128)
+    col, grp = [[1, 128]], [[-16, 8], [0, 16]]
+
+    def ingroup(out, a):
+        keep(out, a, grp, AL.is_ge, 0.0, 0, 1)
+        keep(out, out, [[16, 8], [0, 16]], AL.is_ge, 0.0, 15, -1)
+
+    def corner(out, v):
+        keep(out, out, [[-16, 8], [200, 16]], AL.not_equal, v, 0, 1)
+
     ts(R("q1"), R("iod"), rc, 15.0, AL.add, AL.is_equal)
-    ts(R("ta"), R("iod", 0, 128), rc, 15.0, AL.add, AL.is_le)
-    ts(R("tc"), R("iod", 0, 128), rc, 0.0, AL.add, AL.is_ge)
-    tt(R("bo"), R("ta"), R("tc"), AL.mult)
-    ts(R("tc"), R("iod", 0, 128), 0.0, None, AL.is_ge)
-    tt(R("tri"), R("ta"), R("tc"), AL.mult)
+    ingroup(R("bo"), one)
+    keep(R("tri"), R("bo"), col, AL.is_ge, 0.0, 0, -1)
     ts(R("dmask"), R("j16"), rc, BIG, AL.is_equal, AL.mult)
+    scale(R("c16"), R("c16"), 1.0 / K)
     scale(R("bo16"), R("bo"), 16.0)
+    scale(R("trk"), R("tri"), float(K))
     rng = []
     for b in range(8):
         p0, p1 = (256 * b + 16) / 2048.0, (b + 1) / 8.0
         rng.append((0 if b == 0 else int(256 * p0 / (2 - p0)) // 2 * 2, min(256, int(512 * p1 / (1 + p1)) // 2 * 2 + 2)))
-    z0 = [sum(256 - r[0] for r in rng[:b]) - rng[b][0] for b in range(8)]
-    for x in cfg["order"][0]:
-        for b in range(8):
-            if rng[b][1] < 256:
-                iota(R("zc" + x, z0[b] + rng[b][1], z0[b] + 256), [[0, 256 - rng[b][1]]], 1, 0)
+    z0 = [sum(r[1] - r[0] for r in rng[:b]) - rng[b][0] for b in range(8)]
+    cz = [sum(2 if hi <= c else lo <= c and on == "A" for (lo, hi), on in zip(rng, cfg["zc"])) for c in range(256)]
+    ends = [c for c in range(256) if c == 0 or cz[c] != cz[c - 1]] + [256]
+    for a, b in zip(ends, ends[1:]):
+        act(R("cz", a, b), R("iod", 0, b - a), AF.Identity, bias=float(cz[a]), scale=0.0)
+    scale(R("boh"), R("bo"), 0.5)
+    scale(R("bo8"), R("bo"), 8.0)
     for x in "fb":
         iota(C("o" + x, 0), [[0, 1]], 0, 0)
-        iota(R("st" + x, 128, 136), [[0, 8]], int(MG) + 5000, 0)
-    ts(R("idf"), R("iod", 0, 128), 0.0, None, AL.is_equal)
+        iota(R("st" + x, 1024, 1040), [[0, 16]], int(MG) + 5000, 0)
+    ts(R("idf"), io, 0.0, None, AL.is_equal)
     scale(R("idb"), R("idf"), 1.0)
-    scale(R("ta"), R("idf"), 63.0)
-    tt(R("str"), R("ta"), R("tri"), AL.add)
-    ts(R("ta"), R("iod", 0, 128), 16.0, None, AL.is_equal)
-    ts(R("tc"), R("iod", 0, 128), -112.0, None, AL.is_equal)
-    tt(R("shf"), R("ta"), R("tc"), AL.add)
-    scale(R("shb"), R("shf"), 1.0)
-    ts(C("rc", 1), rc, -16.0, None, AL.add)
-    scale(R("qw"), R("q1"), C("rc", 1))
-    tt(R("qd", 0, 143), R("qw", 0, 143), R("qw", 1, 144), AL.subtract)
-    ts(C("rci", 0), C("rci", 1), 1, None, AL.bitwise_and)
-    ts(C("rc", 2), C("rci", 0), float(WB - 1 - WF), float(WF), AL.mult, AL.add)
+    scale(R("idk"), R("idf"), float(K))
+    scale(R("nid"), R("idf"), -1.0)
+    act(R("w1"), R("j16", 0, 128), AF.Exp, bias=-LN2, scale=-LN2)
+    ingroup(R("w1"), R("w1"))
+    scale(R("nw1"), R("w1"), -1.0)
+    keep(R("b0"), one, grp, AL.is_equal, 0.0, 0, 1)
+    act(R("dl"), R("j16", 0, 128), AF.Exp, bias=-2 * LN2, scale=-LN2)
+    keep(R("dl"), R("dl"), grp, AL.is_equal, 0.0, -1, 1)
+    keep(R("dl"), R("dl"), grp, AL.not_equal, -0.5, 0, 1)
+    scale(R("gg"), R("tri"), -1.0)
+    keep(R("gg"), R("gg"), col, AL.not_equal, -2.0, 0, -1)
+    keep(R("gg"), R("gg"), grp, AL.not_equal, 1.0, 0, 1)
+    corner(R("gg"), 0.0)
+    scale(R("nb0"), R("b0"), -1.0)
+    scale(R("bk"), R("b0"), 1024.0)
+    scale(R("bo512"), R("bo"), PB / 16)
+    keep(R("stt"), R("bo"), col, AL.is_gt, 0.0, 0, -1)
+    keep(R("str"), R("stt"), col, AL.not_equal, 64.0, 0, -1)
+    ms(C("po", 0), -7.5)
+    scale(R("pb0"), R("bo"), 2.0)
+    keep(R("pb0"), R("pb0"), col, AL.is_equal, 0.0, 1, -1)
+    keep(R("pb0"), R("pb0"), col, AL.not_equal, -1.0, 0, -1)
+    for j in range(1, 5):
+        scale(R("pb%d" % j), R("pb0"), 2.0 ** j if j < 4 else PB)
+    for j in range(4):
+        ts(C("rci", 2 + j), C("rci", 1), j, 1, AL.arith_shift_right, AL.bitwise_and)
+    cp(R("rc", 4, 8), R("rci", 2, 6))
+    for j in range(4):
+        scale(R("wb%d" % j), R("w1"), C("rc", 4 + j))
+    keep(R("shb"), one, col, AL.is_equal, 0.0, -16, -1)
+    keep(R("shb"), R("shb"), col, AL.not_equal, 1.0, 112, -1)
+    scale(R("shf"), R("shb"), 1.0)
+    ts(C("rc", 2), C("rc", 4), float(WB - 1 - WF), float(WF), AL.mult, AL.add)
     tt(C("rc", 3), C("rc", 2), rc, AL.add)
-    ts(R("nfill"), R("c16"), C("rc", 3), -1.0, AL.add, AL.mult)
-    ts(R("tbc"), R("tbc"), rc, None, AL.add)
+    ts(C("rc", 8), rc, -6.5, 2 * PB, AL.add, AL.mult)
+    ts(C("rc", 9), C("rc", 3), -1.0, 16.0, AL.mult, AL.add)
+    ts(R("nfill"), R("nc16", 0, 256), C("rc", 9), None, AL.add)
+    ts(R("tbc"), R("tbc"), rc, 16.0, AL.add, AL.mult)
     ts(R("eg"), R("iod", 0, 136), 2.0, rc, AL.mult, AL.add)
     ts(R("ef"), R("eg"), 16.0, -1.0, AL.is_equal, AL.mult)
     ts(R("eg"), R("eg"), 15.0, -1.0, AL.is_equal, AL.mult)
-    for r, v in ((R("k16"), 16), (R("win", 0, 8), 0), (C("po", 0), 0), (C("nn", 0), -8), (R("nn", 256, 280), -8)):
+    for r, v in ((R("win", 0, 16), 0), (C("nn", 0), -8), (R("nn", 256, 280), -8), (R("ok", 256, 258), 1), (R("ok", 257, 272), 0)):
         iota(r, [[0, width(r)]], v, 0)
     cp(R("pia"), R("pis"))
     move(R("pra", 0, 7), R("prb", 0, 7), -1, 28)
@@ -243,8 +297,8 @@ def declare(cfg):
 
     def ancestors(t, x, pool, par, res):
         pr, pn = "pr" + par, "pn" + par
-        bank = "ps4" if x == "b" else "ps7"
-        m0 = 0 if x == "b" else S
+        bank, bk2 = ("ps4", "ps5") if x == "b" else ("ps6", "ps7")
+        m0 = S if x == "b" else 0
         how = cfg["hit"][t][x]
         cw = S // len(how)
         for k, h in enumerate(how):
@@ -252,114 +306,110 @@ def declare(cfg):
             src = [R("mw", m0 + a, m0 + b)]
             if h == "D":
                 ts(src[0], R(pool, a, b), C(pr, t), C(pr, 3), AL.subtract, AL.is_gt)
-                src.append(R("hit", a, b))
+                src.append(R("hit", m0 + a, m0 + b))
                 ts(src[1], R(pool, a, b), C(pr, t), C(pn, 3), AL.subtract, AL.is_lt)
             else:
-                act(R("aw", a, b), R(pool, a, b), AF.Abs, bias=C(pn, t))
-                act(src[0], R("aw", a, b), AF.Relu, bias=C(pn, 4), scale=SC)
-                ts(src[0], R("aw", a, b), C(pr, 3), None, AL.is_gt)
-                either()
-            lst = [(R(bank, a // 16, b // 16), sel(i), (s[0], s[1] + i, s[2], 16)) for s in src for i in range(16)]
-            mm([m + (j == 0, j == len(lst) - 1) for j, m in enumerate(lst)])
+                aw = R("ab", m0 + a, m0 + b)
+                act(aw, R(pool, a, b), AF.Abs, bias=C(pn, t))
+                act(src[0], aw, AF.Relu, bias=C(pn, 4), scale=SC)
+                ts(src[0], aw, C(pr, 3), None, AL.is_gt)
+                either(h)
+            group([(R(bank, a // 16, b // 16), sel(i), (s[0], s[1] + i, s[2], 16)) for s in src for i in range(16)])
         w, o, tq = R("w" + x), "o" + x, "tq" + x
+        tot = C(o, 128)
         ts(w, R(bank, 0, 128), 0.0, 1.0, AL.is_le, AL.add)
-        mm([(R(bank, 256, 384), R("bo"), w, True, True), (R(bank, 128, 256), R("tri"), w, True, True)])
-        scan(R(o, 1, 129), R(bank, 256, 384), R("nb16", 0, 128), 0.0, AL.add, AL.max)
-        ts(C(tq, 0), C(o, 128), 1.0 / K, None, AL.mult)
+        group([(R(bank, 128, 256), R("bo"), w)])
+        scan(R(o, 1, 129), R(bank, 128, 256), R("nc16", 0, 128), 0.0, AL.add, AL.max)
+        cc = R(bank, 256, 384)
+        group([(cc, R("idk"), R(o, 0, 128)), (cc, R("trk"), w)])
+        y, out = R(bank, 0, 256), R(bk2, 0, 256)
+        mm([(y, R("dl"), R("ones", 0, 256), True, False)])
         scan(R("ec" + x), R("dmask", 0, 128), R(o, 1, 129), 0.0, AL.add, AL.min)
-        if cfg["coarse"] == "a":
-            ts(C(tq, 2), C(o, 128), 16.0, None, AL.mult)
-            ts(R("en" + x), R("ec" + x, 15, 128, 16), -65536.0, 128.0, AL.mult, AL.add)
-        bk2 = "ps5" if x == "b" else "ps6"
-        out = R(bk2, 0, 256)
-        for b in range(8):
+        mm([(R(bk2, 256, 512), R("boh"), R("cz"), True, False)])
+        if "A" in cfg["zc"]:
+            act(R("en" + x), R("ec" + x, 15, 128, 16), AF.Identity, bias=1.0 / 512, scale=-1.0)
+        seq = sorted(range(8), key=lambda b: (cfg["zc"][:b].count(cfg["zc"][b]), cfg["zc"][b] == "A"))
+        for b in seq:
             lo, hi = rng[b]
             z = R("zc" + x, z0[b] + lo, z0[b] + hi)
-            ts(z, R("c16", lo, hi), C(tq, 0), C("ec" + x, 16 * b + 15), AL.mult, AL.is_ge)
-            if cfg["coarse"] == "a":
-                act(z, R("c16", lo, hi), AF.Sigmoid, bias=C("en" + x, b), scale=C(tq, 2))
-                either()
-            mm([(R(bk2, 256 + lo, 512), R("bo16"), R("zc" + x, z0[b] + lo, z0[b] + 256), b == 0, b == 7)])
-        add("v", "rcp", (C(tq, 1), C(tq, 0)), [C(tq, 1)], [C(tq, 0)], 250)
-        cc = R(bank, 384, 512)
-        tt(cc, R(o, 0, 128), R(bank, 128, 256), AL.add)
-        if cfg["small"] == "a":
-            act(R("qm" + x), cc, AF.Identity, bias=MG, scale=C(tq, 1))
-        else:
-            ts(R("qm" + x), cc, C(tq, 1), MG, AL.mult, AL.add)
-        ts(R("qt" + x), R("qm" + x), -MG, C(tq, 0), AL.add, AL.mult)
-        tt(R(bank, 0, 128), cc, R("qt" + x), AL.is_gt)
-        tt(R("st" + x, 0, 128), R(bank, 0, 128), R("qm" + x), AL.add)
+            if cfg["zc"][b] == "A":
+                act(z, R("c16", lo, hi), AF.Sign, bias=C("en" + x, b), scale=tot)
+            else:
+                ts(z, R("c16", lo, hi), tot, C("ec" + x, 16 * b + 15), AL.mult, AL.is_ge)
+            mm([(R(bk2, 256 + lo, 256 + hi), R("boh" if cfg["zc"][b] == "A" else "bo"), z, False, b == seq[-1])])
+        add("v", "rcp", (C(tq, 1), tot), [C(tq, 1)], [tot], 250)
+        act(R("qm" + x), cc, AF.Identity, bias=MG, scale=C(tq, 1))
+        ts(R("qm" + x), cc, C(tq, 1), MG, AL.mult, AL.add)
+        either(cfg["qm"])
+        ts(R("qt" + x), R("qm" + x), -MG, tot, AL.add, AL.mult)
+        tt(R(bank, 384, 512), cc, R("qt" + x), AL.is_gt)
+        tt(R("st" + x, 0, 1024, 8), R(bank, 384, 512), R("qm" + x), AL.add)
         scan(R("eb" + x), R("dmask", 0, 256), R(bk2, 256, 512), 0.0, AL.add, AL.min)
-        ts(R("l2" + x, 0, 16), R("eb" + x, 15, 256, 16), 1.0 / 16, None, AL.mult)
-        ts(R("l2" + x, 16, 32), R("eb" + x, 15, 256, 16), 1.0 / 16, 1.0, AL.mult, AL.add)
-        tt(R("x12" + x), ("ind", R("st" + x), R("l2" + x)), R("mc"), AL.subtract)
-        if cfg["q"] == "a":
-            act(R(bank, 0, 256), R("x12" + x, 0, 256), AF.Sigmoid, bias=128.0, scale=-256.0)
-        else:
-            ts(R(bank, 0, 256), R("x12" + x, 0, 256), 0.0, None, AL.is_le)
-        tt(R(bank, 256, 512), R(bank, 0, 256), R("x12" + x, 256, 512), AL.mult)
-        tt(R("xs" + x), R(bank, 256, 512), R("x12" + x, 0, 256), AL.max)
-        act(R("p0" + x), R("x12" + x, 0, 256), AF.Sigmoid, bias=128.0, scale=-256.0)
-        ts(R("p0" + x), R("x12" + x, 0, 256), 0.0, None, AL.is_le)
-        either()
-        mm([(R(bk2, rng[b][0], 256), R("bo16"), R("zc" + x, z0[b] + rng[b][0], z0[b] + 256), b == 0, False) for b in range(8)]
-           + [(out, R("bo"), R("p0" + x), False, False)])
-        for i in range(1, 16):
-            z = R("zz" if x == "b" else "hit", 256 * i, 256 * i + 256)
-            stepf(z, R("xs" + x), i, -1)
-            mm([(out, sel(i), z, False, i == 15)])
+        mm([(out, R("bo8"), R("cz"), True, False)]
+           + [(R(bk2, lo, hi), R("bo8" if cfg["zc"][b] == "A" else "bo16"), R("zc" + x, z0[b] + lo, z0[b] + hi), False, False)
+              for b, (lo, hi) in enumerate(rng)])
+        ts(R("l2" + x), R("eb" + x, 15, 256, 16), 8.0, None, AL.mult)
+        for h in range(2):
+            a, b = 256 * h, 256 * h + 256
+            tt(R("x12" + x, a, b), ("ind", R("st" + x, 8 * h, 8 * h + 1032), R("l2" + x)), R("mc"), AL.subtract)
+            ts(R("xc" + x, a, b), R("x12" + x, a, b), 0.0, 16.0, AL.max, AL.min)
+            act(R("xe" + x, a, b), R("xc" + x, a, b), AF.Exp, scale=LN2)
+            if h == 0:
+                ts(R("p0" + x), R("x12" + x, 0, 256), 0.0, None, AL.is_le)
+                act(R("p0" + x), R("xc" + x, 0, 256), AF.Relu, bias=1.0, scale=-1.0)
+                either(cfg["p0"])
+                mm([(y, R("nw1"), R("p0" + x), False, False), (out, R("bo"), R("p0" + x), False, False)])
+            mm([(y, R("w1"), R("xe" + x, a, b), False, h == 1)])
+        ts(R("xf" + x), y, MG, MG, AL.add, AL.subtract)
+        mm([(out, R("gg"), R("xf" + x), False, True)])
         cp(R(res), out)
 
-    def filling(t, a, b):
-        h = b == 256
-        e = b + 16 * h
-        if t < 2 and cfg["small"] == "a":
-            act(R("ok", a, b), R("ps7", a, b), AF.Sigmoid, bias=7.5 * 256, scale=-256.0)
-        else:
-            ts(R("ok", a, b), R("ps7", a, b), 7.5, None, AL.is_le)
-        ex, cs = R("ps4", a, b), R("ps4", 256 + a, 256 + b)
-        mm([(cs, R("bo"), R("ok", a, b), True, True), (ex, R("str"), R("ok", a, b), True, True)])
-        scan(R("po", a + 1, b + 1), cs, R("nb16", a, b), C("po", a), AL.add, AL.max)
-        if h:
-            ts(R("po", 257, 273), R("k16"), C("po", 256), None, AL.add)
-        cp(R("oi", a, e), R("po", a, e))
-        ts(R("pa", a, e), R("oi", a, e), 15, None, AL.bitwise_and)
-        tt(R("px", a, b), ex, R("pa", a, b), AL.add)
-        ts(R("py", a, b), R("px", a, b), 79, None, AL.bitwise_and)
-        cp(R("pc", a, b), R("py", a, b))
-        v = R("ps6", a, b)
-        for i in range(16):
-            z = R("zz", 256 * i + a, 256 * i + b)
-            if t < 2:
-                stepf(z, R("pc", a, b), 64 + i, 1)
-            else:
-                ts(z, R("pc", a, b), 64.0 + i, None, AL.is_ge)
-            mm([(v, R("qd" if i else "qw", 15 - i, 143 - i), z, i == 0, i == 15)])
-        ts(R("pg", a, e), R("pa", a, e), rc, BIG, AL.is_le, AL.mult)
-        w = e - a
-        for k in range(2):
-            scan(R("pe", 2 * a + k * w, 2 * a + k * w + w), R("dmask", a, e), R("po", a + k, e + k), 0.0, AL.add, AL.min)
-        k0, k1, k2 = a // 8, a // 8 + w // 16, a // 8 + w // 8
-        ts(R("pk2", k0, k2), R("pe", 2 * a + 15, 2 * e, 16), 1.0 / 16, -15.0 / 32, AL.mult, AL.add)
+    def filling(t, j, a, b):
+        e = b + 16 * (b == 256)
+        w, v = b - a, e - a
+        pb = "ps5" if j % 2 else "ps6"
+        arg, xr, n0 = R(pb, 2 * v, 2 * v + w), R("ps7", 256, 256 + v), R("ps7", 0, v + 1)
+        ts(R("ok", a, b), R("ps4", a, b), 7.5, None, AL.is_le)
+        group([(R(pb, 0, v), R("bo"), R("ok", a, e))])
+        scan(R("po", a + 1, e + 1), R(pb, 0, v), R("nc16", 0, v), C("po", a), AL.add, AL.max)
+        group([(n0, R("idf"), R("po", a, e + 1)), (R("ps7", 0, v), R("stt"), R("ok", a, e))])
+        mm([(arg, R("idf"), R("po", a, b), True, False), (arg, R("str"), R("ok", a, b), False, False)])
+        ts(R("f16", a, e + 1), n0, M16, M16, AL.add, AL.subtract)
+        mm([(arg, R("nid"), R("f16", a, b), False, True)])
+        act(R("ee", a, b), arg, AF.Exp, bias=LN2 * (8.5 - 64), scale=LN2)
+        group([(xr, R("idf"), R("po", a, e)), (xr, R("nb0"), R("f16", a, e))])
+        for h in range(0, 5 * w, 512):
+            top = min(5 * w, h + 512)
+            mm([(R("psb", h, top), R("dl"), R("ones", 0, top - h), True, False)])
+            lst = []
+            for k, mat in enumerate(("wb0", "wb1", "wb2", "wb3", "w1")):
+                lo, hi = max(h, k * w), min(top, k * w + w)
+                if lo < hi:
+                    lst.append((R("psb", lo, hi), R(mat), R("ee", a + lo - k * w, a + hi - k * w), False, hi == top))
+            mm(lst)
+            ts(R("ff", 5 * a + h, 5 * a + top), R("psb", h, top), MG, MG, AL.add, AL.subtract)
+        s1, s2, pg = R(pb, 0, v), R(pb, v, 2 * v), R(pb, 2 * v, 3 * v)
+        group([(s1, R("bk"), R("f16", a, e)), (s1, R("b0"), R("f16", a, e))])
+        group([(s2, R("bk"), R("f16", a + 1, e + 1))])
+        act(pg, xr, AF.Relu, bias=C("rc", 8), scale=-2 * PB)
+        if e > b:
+            ts(C("nn", 257), C(pb, v + w - 1), -1.0 / 1024, C("rc", 3), AL.mult, AL.subtract)
+        scan(R("pe", 2 * a, 2 * e), R("dmask", 0, 2 * v), R(pb, 0, 2 * v), 0.0, AL.add, AL.min)
         q, q2 = R("pq", a // 16, e // 16), R("pq2", a // 16, e // 16)
-        tt(q, R("pk2", k0, k1), R("pk2", k1, k2), AL.is_equal)
-        tt(q2, q, R("tbc", a // 16, e // 16), AL.mult)
-        tt(q, q2, R("pk2", k0, k1), AL.add)
-        cp(R("pl", a // 16, e // 16), q)
-        if cfg["small"] == "a":
-            act(R("d0", a, b), v, AF.Identity, scale=BIG)
-        else:
-            ts(R("d0", a, b), v, BIG, None, AL.mult)
-        tt(R("t1", a, b), R("nb16", a, b), v, AL.subtract)
-        scan(R("nn", a + 1, b + 1), R("d0", a, b), R("t1", a, b), C("nn", a), AL.add, AL.max)
-        if h:
-            ts(C("nn", 257), C("pa", 256), C("po", 256), C("rc", 3), AL.subtract, AL.subtract)
-        tt(R("yy", a, e), R("nn", a, e), R("pg", a, e), AL.subtract)
+        tt(q, R("pe", 2 * a + 15, 2 * a + v, 16), R("pe", 2 * a + v + 15, 2 * e, 16), AL.subtract)
+        tt(q2, q, R("tbc", a // 16, e // 16), AL.min)
+        ts(R("pl", a // 16, e // 16), q2, 1.0 / 16, 1024.0, AL.mult, AL.add)
+        arg = R(pb, 0, w)
+        mm([(arg, R("idb"), R("nc16", a, b), True, False), (arg, R("bo512"), R("ones", 0, w), False, False)])
+        for k in range(5):
+            mm([(arg, R("pb%d" % k), R("ff", 5 * a + k * w, 5 * a + (k + 1) * w), False, k == 4)])
+        scan(R("nn", a + 1, b + 1), arg, R("dmask", 0, w), C("nn", a), AL.min, AL.min)
+        tt(R("yy", a, e), R("nn", a, e), pg, AL.subtract)
         tt(("ind", R("pw"), R("pl", a // 16, e // 16)), R("nn", a + 1, e + 1), R("yy", a, e), AL.max)
 
     pools = [{"f": "f0s", "b": "b0s"}, {"f": "fp1", "b": "lb"}, {"f": "lf", "b": "lb"}]
     dest = [{"f": "fp1", "b": "sb0"}, {"f": "sf1", "b": "lb"}, {"f": "fp1", "b": "lb"}]
+    ub = [("psa", 0), ("psa", 512), ("psb", 0), ("psb", 512)]
     for t in range(3):
         par = "b" if t == 1 else "a"
         pr, pn = "pr" + par, "pn" + par
@@ -374,52 +424,65 @@ def declare(cfg):
                 ancestors(t, x, dest[t - 1][x], "c" if t == 1 else "d", "sa" + x)
                 move(R("sa" + x), R(al[x]), -2 if t == 1 else 2, 512)
         bias[0] = 0.0
-        cw = K // cfg["bA"]
-        for k in range(cfg["bA"]):
-            gather(R("win", WB + k * cw, WB + (k + 1) * cw), R(pools[t]["b"]), R(al["b"], k * cw // 16, (k + 1) * cw // 16))
-        a = 0
-        for k, cw in enumerate(cfg["gch"]):
+        cw = K // len(cfg["bA"][t])
+        bias[0] = cfg["ba"][t]
+        for k, on in enumerate(cfg["bA"][t]):
+            a, b = k * cw, (k + 1) * cw
+            gather(R("win", WB + a, WB + b), R(pools[t]["b"], 0, reach(b)), R(al["b"], a // 16, b // 16), on)
+        bias[0] = 0.0
+        a = done = 0
+        for k, cw in enumerate(cfg["gch"][t]):
             b = a + cw
-            fi, d, m = R("win", WF + a, WF + b), R("dd", a, b), R("win", WM + a, WM + b)
-            e = R("psa" if k % 2 == 0 else "psb", 0, cw)
-            gather(fi, R(pools[t]["f"]), R(al["f"], a // 16, b // 16))
-            tt(d, ("ind", R("win", WB, WW), R("pi" + par, a // 16, b // 16)), fi, AL.subtract)
-            act(e, d, AF.Identity, scale=C(pr, 4))
-            tt(m, fi, e, AL.add)
-            act(R("ab", a, b), m, AF.Abs, bias=C(pn, t))
+            bias[0] = cfg["slope"] * (K - a)
+            gather(R("win", WF + a, WF + b), R(pools[t]["f"], 0, reach(b)), R(al["f"], a // 16, b // 16), cfg["fi"][t][k])
+            tt(R("dd", a, b), ("ind", R("win", WB, WW), R("pi" + par, a // 16, b // 16)), R("win", WF + a, WF + b), AL.subtract)
+            for c in range(a, b, 512):
+                c1 = min(b, c + 512)
+                e = R("psa", c % 1024, c % 1024 + c1 - c)
+                scale(e, R("dd", c, c1), C(pr, 4), "A")
+                tt(R("win", WM + c, WM + c1), R("win", WF + c, WF + c1), e, AL.add)
+            act(R("ab", a, b), R("win", WM + a, WM + b), AF.Abs, bias=C(pn, t))
             if cfg["acc"][t][k] == "V":
                 ts(R("hit", a, b), R("ab", a, b), C(pr, 3), None, AL.is_gt)
             else:
                 act(R("hit", a, b), R("ab", a, b), AF.Relu, bias=C(pn, 4), scale=SC)
                 act(R("hit", a, b), R("hit", a, b), AF.Sign)
                 ts(R("hit", a, b), R("hit", a, b), 0.0, None, AL.is_gt)
-                either()
-            mm([(R("ps7", a // 16, b // 16), sel(i), R("hit", a + i, b, 16), i == 0, i == 15) for i in range(16)])
+                either("A" if cfg["acc"][t][k] == "A" else "V")
+            if b - done >= 1024 or b // 16 in cfg["parts"][t]:
+                group([(R("ps4", done // 16, b // 16), sel(i), R("hit", done + i, b, 16)) for i in range(16)])
+                done = b
             if t == 2:
-                act(R("tb", a, b), d, AF.Square)
+                bias[0] = cfg["ye"]
+                act(R("tb", a, b), R("dd", a, b), AF.Square)
                 act(R("tb", a, b), R("tb", a, b), AF.Exp, scale=-1.0)
                 for z in range(a, b, 256):
-                    mm([(R("ps5", 0, 256), R("idf"), R("tb", z, z + 256), z == 0, z == K - 256)])
-            if b // 16 in cfg["parts"]:
-                j = cfg["parts"].index(b // 16)
-                bias[0] = cfg["bp"]
-                filling(t, cfg["parts"][j - 1] if j else 0, b // 16)
+                    mm([(R("psb", 512, 768), R("idf"), R("tb", z, z + 256), z == 0, z == K - 256)])
+                bias[0] = 0.0
+            parts = cfg["parts"][t]
+            if b // 16 in parts:
+                j = parts.index(b // 16)
+                bias[0] = cfg["bp"][j]
+                filling(t, j, parts[j - 1] if j else 0, b // 16)
                 bias[0] = 0.0
             a = b
         if t == 2:
-            act(R("yes"), R("ps5", 0, 256), AF.Copy)
+            act(R("yes"), R("psb", 512, 768), AF.Copy)
             dma("s", ("hbm", "ye", 0, 256), R("yes"), 1024)
         seq = cfg["step"][t]
         for x in (seq[0], "f" if seq[0] == "b" else "b"):
             j = 0 if x == "f" else 1
-            u, mat = R("ps7" if j else "ps4", 0, 128), "eg" if j else "ef"
-            mm([(u, R(mat, 8, 136), R("pw", 0, 256, 2), True, False), (u, R(mat, 0, 128), R("pw", 1, 256, 2), False, True)])
-            cp(R("ll", 128 * j, 128 * j + 128), u)
+            mat = "eg" if j else "ef"
+            for a, b in (((0, 64), (64, 128)) if x == seq[0] else ((0, 128),)):
+                u = R(("ps6", "ps7", "ps4")[(a > 0) + 2 * (x != seq[0])], a, b)
+                group([(u, R(mat, 8, 136), R("pw", 2 * a, 2 * b, 2)), (u, R(mat, 0, 128), R("pw", 2 * a + 1, 2 * b, 2))])
+                cp(R("ll", 128 * j + a, 128 * j + b), u)
         pos = {"f": 0, "b": 0}
-        for k, x in enumerate(seq):
+        nb = 0
+        for x in seq:
             j = 0 if x == "f" else 1
-            bias[0] = cfg["s" + x][t]
             sa = sum(cfg["sch"][t][:pos[x]])
+            bias[0] = cfg["s" + x][t] + cfg["slope2"] * (S - sa)
             cw = cfg["sch"][t][pos[x]]
             sb = sa + cw
             pos[x] += 1
@@ -427,23 +490,31 @@ def declare(cfg):
             src = ("ind", R("win"), R("ll", a // 16, b // 16))
             act(R("ab", a, b), src, AF.Square)
             tt(R("dd", a, b), src, R("ab", a, b), AL.subtract)
-            u = R("psa" if k % 4 < 2 else "psb", 512 * (k % 2), 512 * (k % 2) + cw)
             mat = "sh" if x == "b" and t < 2 else "id"
-            if mat == "sh" or cfg["nzp"][t][k] == "P":
-                scale(R("tb", a, b), R("dd", a, b), C(pr, 5 + j))
-                mm([(u, R(mat + "f"), R("tb", a, b), True, False), (u, R(mat + "b"), R("nz" + par, sa, sb), False, True)])
+            if cw > 512 and nb % 2:
+                nb += 1
+            un, u0 = ub[nb % 4]
+            cuts = [(c, min(cw, c + 512)) for c in range(0, cw, 512)]
+            nb += len(cuts)
+            if mat == "sh":
+                scale(R("tb", a, b), R("dd", a, b), C(pr, 5 + j), "A")
+                for c, c1 in cuts:
+                    u = R(un, u0 + c, u0 + c1)
+                    group([(u, R("shf"), R("tb", a + c, a + c1)), (u, R("shb"), R("nz" + par, sa + c, sa + c1))])
             else:
-                act(u, R("dd", a, b), AF.Identity, scale=C(pr, 5 + j))
-                tt(R("tb", a, b), u, R("nz" + par, sa, sb), AL.add)
-                u = R("tb", a, b)
+                mm([(R(un, u0 + c, u0 + c1), R("idb"), R("ones", 0, c1 - c), True, False) for c, c1 in cuts])
+                scale(R(un, u0, u0 + cw), R("dd", a, b), C(pr, 5 + j), "A")
+                mm([(R(un, u0 + c, u0 + c1), R("idb"), R("nz" + par, sa + c, sa + c1), False, True) for c, c1 in cuts])
             new = R(dest[t][x], sa, sb)
-            ts(new, u, 0.0, 1.0, AL.max, AL.min)
+            ts(new, R(un, u0, u0 + cw), 0.0, 1.0, AL.max, AL.min)
             if t == 2:
                 dma("s", ("hbm", "y" + x, sa, sb), new, 4 * cw)
-            elif t == 0 and x == "b":
-                move(new, R("lb", sa, sb), -2, 4 * cw)
-            elif t == 1 and x == "f":
-                move(new, R("lf", sa, sb), 2, 4 * cw)
+            elif x == "bf"[t]:
+                way = cfg["way"][t][pos[x] - 1]
+                mid = {"D": sb, "R": sa, "S": (sa + sb) // 2}[way]
+                for c, c1, via in ((mid, sb, True), (sa, mid, False)):
+                    if c < c1:
+                        move(R(dest[t][x], c, c1), R("l" + x, c, c1), 4 * t - 2, 4 * (c1 - c), via)
     return ops
 
 
@@ -466,7 +537,7 @@ def prepare(cfg):
         bk = set(b for a in o["rd"] + o["wr"] if a[0] in PS for b in banks(a))
         for b in bk:
             prev, cur = last.get(b, ([], []))
-            if cur and ops[cur[-1]]["eng"] != o["eng"]:
+            if cur and (ops[cur[-1]]["eng"] != o["eng"] or ops[cur[-1]]["alt"] or o["alt"]):
                 prev, cur = cur, []
             dep.update(prev)
             if cur and o["eng"] == "p":
@@ -486,15 +557,13 @@ def prepare(cfg):
     pri = [0.0] * n
     for i in range(n - 1, -1, -1):
         pri[i] = ops[i]["cost"] + max([pri[j] + cfg["lat"] for j in succ[i]], default=0.0)
-    rs = np.random.RandomState(cfg["seed"])
-    pri = [p + o["bias"] + cfg["noise"] * float(x) for p, o, x in zip(pri, ops, rs.rand(n))]
-    return ops, succ, pri
+    return ops, succ, [p + o["bias"] for p, o in zip(pri, ops)]
 
 
-def schedule(cfg, ops, succ, pri, nudge):
+def schedule(cfg, ops, succ, pri):
     n = len(ops)
     free = dict((e, 0.0) for e in "vapgsx")
-    link = 0.0
+    link = [0.0, 0.0]
     done, start, took = [0.0] * n, [0.0] * n, [False] * n
     left = [len(o["dep"]) for o in ops]
     at = [0.0] * n
@@ -502,11 +571,9 @@ def schedule(cfg, ops, succ, pri, nudge):
 
     def offer(i):
         o = ops[i]
-        d, f = nudge.get(i, (0, 0))
-        if f != 2 or not o["alt"]:
-            ready[o["eng"]][i] = pri[i] + 100.0 * d
-        if f != 1 and o["alt"]:
-            ready[o["alt"][0]][i] = pri[i] + 100.0 * d - cfg["p" + o["alt"][0]]
+        ready[o["eng"]][i] = pri[i]
+        if o["alt"]:
+            ready[o["alt"][0]][i] = pri[i] - cfg["p" + o["alt"][0]]
 
     for i in range(n):
         if left[i] == 0:
@@ -518,11 +585,13 @@ def schedule(cfg, ops, succ, pri, nudge):
             c = ready[e]
             if c:
                 t0 = max(free[e], min(at[i] for i in c))
-                if best is None or t0 <= best[0][0]:
-                    i = max((c[i], -i) for i in c if at[i] <= t0 + 1)[1]
-                    key = (t0, ops[-i]["eng"] != e)
-                    if best is None or key < best[0]:
-                        best = (key, -i, e)
+                p, i = max((c[i], -i) for i in c if at[i] <= t0 + 1)
+                p2, i2 = max((c[j], -j) for j in c if at[j] <= t0 + 1 + min(cfg["wait"], 0.5 * ops[-i]["cost"]))
+                if p2 > p + cfg["gap"]:
+                    t0, i = at[-i2], i2
+                key = (t0, ops[-i]["eng"] != e)
+                if best is None or key < best[0]:
+                    best = (key, -i, e)
         (t0, alt), i, e = best
         o = ops[i]
         took[i] = alt
@@ -533,7 +602,8 @@ def schedule(cfg, ops, succ, pri, nudge):
             free[e] = t0 + 60; done[i] = t0 + o["cost"]
         elif o["kind"] == "rem":
             free[e] = t0 + 500
-            done[i] = link = max(link, t0 + 2500) + o["cost"] - 2500
+            via = o["args"][4]
+            done[i] = link[via] = max(link[via], t0 + o["pre"]) + o["cost"] - o["pre"]
         else:
             done[i] = free[e] = t0 + (o["alt"][3] if alt else o["cost"])
         start[i] = t0
@@ -546,13 +616,52 @@ def schedule(cfg, ops, succ, pri, nudge):
     return order, took, start, done
 
 
+def justify(cfg, ops, succ, done):
+    n = len(ops)
+    shape = []
+    for o in ops:
+        if o["kind"] == "dma":
+            shape.append((o["eng"], 0.0, 60.0, o["cost"] - 60))
+        elif o["kind"] == "rem":
+            shape.append(("link%d" % o["args"][4], o["pre"], o["cost"] - o["pre"], 0.0))
+        else:
+            shape.append((o["eng"], 0.0, 0.0 if o["eng"] == "x" else o["cost"], 1.0))
+
+    def place(key, before, back):
+        start, end, busy = [0.0] * n, [0.0] * n, {}
+        for i in sorted(range(n), key=lambda i: (-key[i], -i if back else i)):
+            res, pre, dur, post = shape[i]
+            if back:
+                pre, post = post, pre
+            t = pre + max([end[j] + (0 if res == "p" == shape[j][0] else cfg["lat"]) for j in before[i]], default=0.0)
+            lst = busy.setdefault(res, [])
+            k = len(lst)
+            while k and lst[k - 1][1] > t:
+                k -= 1
+            while k < len(lst) and lst[k][0] < t + dur:
+                t = max(t, lst[k][1]); k += 1
+            lst.insert(k, (t, t + dur))
+            start[i], end[i] = t - pre, t + dur + post
+        return start, end
+
+    best = None
+    for _ in range(cfg["passes"]):
+        start, done = place(place(done, succ, True)[1], [o["dep"] for o in ops], False)
+        if best is None or max(done) < max(best[1]):
+            best = (start, done)
+    return sorted(range(n), key=lambda i: (best[0][i], i)), best[0], best[1]
+
+
 def plan(cfg):
     ops, succ, pri = prepare(cfg)
-    order, took, start, done = schedule(cfg, ops, succ, pri, cfg["nudge"])
+    order, took, start, done = schedule(cfg, ops, succ, pri)
     for i, o in enumerate(ops):
-        o["took"], o["t0"], o["t1"] = took[i], start[i], done[i]
         if took[i]:
             o["eng"], o["kind"], o["args"], o["cost"] = o["alt"]
+    if cfg["passes"]:
+        order, start, done = justify(cfg, ops, succ, done)
+    for i, o in enumerate(ops):
+        o["took"], o["t0"], o["t1"] = took[i], start[i], done[i]
     count = dict((e, 0) for e in "vapg")
     known = dict((e, {}) for e in "vapgsx")
     for i in order:
@@ -593,11 +702,6 @@ SEMAPHORES = ["cv", "ca", "cp", "cg", "ls"] + [o["sem"] for o in OPS if o["kind"
 
 
 def rank_program(g, core, T, topo):
-    rank = T.rank_of(core)
-    if rank is None:
-        return
-    q = {"v": g.vector, "a": g.scalar, "p": g.tensor, "g": g, "s": g.sync}
-
     def ap(a):
         if not isinstance(a, tuple):
             return a
@@ -607,10 +711,38 @@ def rank_program(g, core, T, topo):
             return T[a[1]][:] if a[3] - a[2] == T[a[1]].shape[1] else T[a[1]][:, a[2]:a[3]]
         return T[a[0]][:, a[1]:a[2]] if a[3] == 1 else T[a[0]][:, a[1]:a[2]:a[3]]
 
+    def helper(r):
+        c = T.cores[r]
+        far = [T.cores[(r + o["args"][2]) % N] for o in OPS if o["kind"] == "rem" and o["args"][4]]
+        return [h for h in topo.cores_of(c) if topo.die(h) != topo.die(c) and T.rank_of(h) is None
+                and all(topo.may_write(h, d) for d in far)][0]
+
+    def spare(r, dst):
+        c = T.cores[r]
+        return [e for e in topo.engines(c, helper(r)) if e not in topo.engines(c, dst)]
+
+    rank = T.rank_of(core)
+    if rank is None:
+        sent = 0
+        for r in range(N):
+            if helper(r) == core:
+                for i in ORDER:
+                    a = OPS[i]["args"]
+                    if OPS[i]["kind"] == "rem" and a[4]:
+                        dst = T.cores[(r + a[2]) % N]
+                        rid, pid, _ = topo.addr(dst)
+                        g.wait_ge(T.sem[a[3]], len(spare(r, dst)))
+                        g.remote_dma(ap(a[1]), ap(a[1]), T.sem[a[3]], T.sem.ls, pid, rid, topo.mask(core, dst))
+                        sent += len(topo.engines(core, dst))
+        if sent:
+            g.wait_ge(T.sem.ls, sent)
+        return
+    q = {"v": g.vector, "a": g.scalar, "p": g.tensor, "g": g, "s": g.sync}
     arrive = {}
     for o in OPS:
         if o["kind"] == "rem":
-            arrive[o["args"][3]] = len(topo.engines(T.cores[(rank - o["args"][2]) % N], core))
+            src = (rank - o["args"][2]) % N
+            arrive[o["args"][3]] = len(topo.engines(helper(src) if o["args"][4] else T.cores[src], core))
     sent = 0
     for i in ORDER:
         o = OPS[i]
@@ -621,9 +753,10 @@ def rank_program(g, core, T, topo):
             e.wait_ge(T.sem[s], arrive.get(s, val))
         if k == "rem":
             dst = T.cores[(rank + a[2]) % N]
-            rid, pid, _ = topo.addr(dst)
-            g.remote_dma(ap(a[1]), ap(a[0]), T.sem[a[3]], T.sem.ls, pid, rid, topo.mask(core, dst))
-            sent += len(topo.engines(core, dst))
+            use = spare(rank, dst) if a[4] else topo.engines(core, dst)
+            rid, pid, _ = topo.addr(helper(rank) if a[4] else dst)
+            g.remote_dma(ap(a[1]), ap(a[0]), T.sem[a[3]], T.sem.ls, pid, rid, sum(1 << x for x in use))
+            sent += len(use)
             continue
         if k == "dma":
             e.dma_start(ap(a[0]), ap(a[1])).then_inc(T.sem[o["sem"]], 16)
@@ -642,6 +775,8 @@ def rank_program(g, core, T, topo):
             ins = [e.memset(ap(a[0]), a[1])]
         elif k == "rcp":
             ins = [e.reciprocal(ap(a[0]), ap(a[1]))]
+        elif k == "sel":
+            ins = [e.affine_select(ap(a[0]), ap(a[1]), *a[2:])]
         elif k == "iota":
             if dty(a[0]) == I:
                 ins = [e.iota(ap(a[0]), a[1], a[2], a[3])]

import math
from concourse.mybir import AluOpType, ActivationFunctionType

AL = AluOpType
AF = ActivationFunctionType
S, K, N = 2048, 4096, 8
MG = 12582912.0
M16 = 16 * MG
BIG = 2.0 ** 26
PB = 8192.0
SC = 2.0 ** 60
LN2 = math.log(2.0)
WM, WF, WB, WW = 16, 16 + K, 16 + 2 * K, 16 + 3 * K

F, H, I, U = "float32", "bfloat16", "int32", "uint16"
SCRATCH = {}
for _n, _w, _d in [
    ("f0s", S, H), ("b0s", S, H), ("nza", S, H), ("nzb", S, H), ("pis", 256, I), ("pia", 256, U), ("pib", 256, U),
    ("pra", 8, F), ("prb", 8, F), ("pna", 8, F), ("pnb", 8, F), ("prc", 8, F), ("prd", 8, F), ("pnc", 8, F), ("pnd", 8, F),
    ("sab", 256, U), ("saf", 256, U), ("lab", 256, U), ("laf", 256, U),
    ("win", WW, F), ("dd", K, F), ("ab", K, F), ("tb", K, F), ("hit", K, H), ("mw", 2 * S, H),
    ("fp1", S, F), ("sb0", S, F), ("lb", S, F), ("sf1", S, F), ("lf", S, F), ("yes", 256, F),
    ("zcf", 768, H), ("zcb", 768, H), ("cz", 256, H), ("ef", 136, F), ("eg", 136, F),
    ("iod", 144, F), ("rci", 8, I), ("rc", 12, F), ("j16", 416, F), ("dmask", 416, F), ("c16", 256, H), ("mc", 256, F),
    ("nc16", 272, H), ("ones", 512, H), ("nfill", 256, F), ("tbc", 17, F),
    ("q1", 144, H), ("mh", 128 * 22, H), ("mf", 128 * 9, F),
    ("ok", 272, H), ("po", 280, F), ("f16", 288, H), ("ee", 256, H), ("ff", 1280, F), ("pe", 544, F), ("pq", 18, F),
    ("pq2", 18, F), ("pl", 18, U), ("nn", 280, F), ("yy", 272, F), ("pw", 576, F), ("ll", 256, U),
]:
    SCRATCH[_n] = ("sbuf", [128, _w], _d)
for _x in "fb":
    for _n, _w, _d in [("w", 128, H), ("o", 136, F), ("tq", 4, F), ("en", 8, F), ("qm", 128, F), ("qt", 128, F), ("st", 1040, F),
                       ("ec", 128, F), ("eb", 256, F), ("l2", 16, U), ("x12", 512, H), ("xc", 512, H), ("xe", 512, H),
                       ("p0", 256, H), ("xf", 256, F), ("al", 256, U)]:
        SCRATCH[_n + _x] = ("sbuf", [128, _w], _d)
PS = {"psa": (1024, 0), "psb": (1024, 2), "ps4": (512, 4), "ps5": (512, 5), "ps6": (512, 6), "ps7": (512, 7)}
for _n in PS:
    SCRATCH[_n] = ("psum", [128, PS[_n][0]], F)
MH = ["bo", "bo16", "bo512", "tri", "trk", "str", "stt", "idb", "nid", "shb", "w1", "nw1", "wb0", "wb1", "wb2", "wb3",
      "dl", "b0", "nb0", "bk", "boh", "bo8"]
MF = ["idf", "idk", "shf", "gg", "pb0", "pb1", "pb2", "pb3", "pb4"]

CFG = {
    "gch": [[512, 1024, 1024, 512, 512, 512]] * 3,
    "parts": [[96, 192, 256]] * 3,
    "sch": [[512, 512, 1024], [512, 512, 1024], [1024, 512, 512]],
    "step": ["bbbfff", "fffbbb", "bfbfbf"],
    "hit": [{"b": "DD", "f": "AA"}, {"f": "AA", "b": "AA"}, {"b": "AA", "f": "AA"}],
    "order": ["bf", "bf", "fb"],
    "bA": ["AVAV"] * 3, "fi": ["AAAAAAAA"] * 3, "acc": ["VVVVVVVV"] * 3, "qm": "A", "p0": "V",
    "ba": [0.0, 0.0, 0.0], "ye": 0.0, "wait": 300.0, "gap": 500.0, "slope": 1.0, "slope2": 1.0, "passes": 3,
    "sf": [0.0, 0.0, 0.0], "sb": [0.0, 0.0, 0.0], "bb": [0.0, 0.0, 0.0], "bf": [0.0, 0.0, 0.0], "bp": [3000.0, 0.0, 0.0, 0.0],
    "pv": 0.0, "pa": 3000.0,
    "way": ["DRDSD", "DRDSD"], "zc": "VAVAVAVA",
    "g": 1.56, "sc": 3.8, "pe": 0.55, "lat": 160.0, "fix": 60.0, "link": 50.0, "hop": 100.0,
}
CFG.update({
    'gch': [[512, 512, 1024, 1024, 512, 512], [512, 1024, 1024, 512, 512, 512], [512, 1024, 1024, 512, 512, 512]],
    'parts': [[64, 192, 256], [96, 192, 256], [96, 192, 256]],
    'sch': [[512, 512, 512, 512], [256, 768, 512, 512], [512, 512, 512, 256, 256]], 'step': ['bfbfbfbf', 'fbffbfbb', 'bbbbbfffff'],
    'hit': [{'b': 'AV', 'f': 'DD'}, {'f': 'AA', 'b': 'VV'}, {'b': 'AA', 'f': 'VV'}], 'order': ['fb', 'fb', 'bf'],
    'bA': ['AVAV', 'AVAV', 'AVAV'], 'fi': ['AVAAAVVA', 'VAAAAAAV', 'VAVAAAVA'], 'acc': ['VVBVVVVB', 'BVVAVVVV', 'VVVAVVVA'],
    'qm': 'A', 'p0': 'V', 'ba': [-6000.0, -3000.0, 0.0], 'ye': -10000.0, 'wait': 300.0, 'gap': 2000.0, 'slope': 0.5,
    'slope2': 0.5, 'passes': 1, 'sf': [500.0, -1500.0, 500.0], 'sb': [500.0, 0.0, 1500.0], 'bb': [-1500.0, 1500.0, 0.0],
    'bf': [-3000.0, 0.0, -1500.0], 'bp': [3000.0, 6000.0, 6000.0, 0.0], 'pv': 5000.0, 'way': ['DSRSD', 'SDDRS'], 'zc': 'AVAVAVAV'})


def width(a):
    if a[0] == "ind":
        return 16 * (a[2][2] - a[2][1])
    return (a[2] - a[1] + a[3] - 1) // a[3]


def dty(a):
    return SCRATCH[a[1][0] if a[0] == "ind" else a[0]][2]


def R(n, a=0, b=None, s=1):
    if n in MH or n in MF:
        j = 128 * (MH.index(n) if n in MH else MF.index(n))
        return ("mh" if n in MH else "mf", j, j + 128, 1)
    return (n, a, SCRATCH[n][1][1] if b is None else b, s)


def C(n, j):
    return (n, j, j + 1, 1)


def declare(cfg):
    ops = []

    def add(eng, kind, args, outs, ins, cost, sem=None, after=None):
        rd, wr = [], []
        for a in ins:
            if isinstance(a, tuple):
                rd.extend([a[1], a[2]] if a[0] == "ind" else [a])
        for a in outs:
            if a[0] == "ind":
                wr.append(a[1]); rd.append(a[2])
            else:
                wr.append(a)
        ops.append({"eng": eng, "kind": kind, "args": args, "rd": rd, "wr": wr, "cost": cost, "sem": sem,
                    "after": after, "n": len(args) if kind == "mm" else 1, "alt": None, "bias": bias[0]})
        return len(ops) - 1

    bias = [0.0]

    def either(on="?"):
        b = ops.pop()
        a = ops[-1]
        if on == "?":
            a["alt"] = (b["eng"], b["kind"], b["args"], b["cost"])
            a["rd"] = a["rd"] + b["rd"]
        elif on.lower() == b["eng"]:
            ops[-1] = b

    def cyc(out, in0, base):
        n = width(in0)
        if out[0] == "ind":
            return cfg["fix"] + cfg["sc"] * n
        if in0[0] == "ind":
            return cfg["fix"] + cfg["g"] * n
        if base == 1 and dty(out) in (H, U) and dty(in0) in (H, U):
            base = 0.5
        return cfg["fix"] + max(64, base * n)

    def ts(out, in0, s1, s2, o0, o1=None):
        add("v", "ts", (out, in0, s1, s2, o0, o1), [out], [in0, s1, s2], cyc(out, in0, 1))

    def tt(out, a, b, op):
        add("v", "tt", (out, a, b, op), [out], [a, b], cyc(out, a, 1.01 if a[0] in PS or b[0] in PS else 2))

    def cp(out, a):
        add("v", "cp", (out, a), [out], [a], cyc(out, a, 1))

    def scan(out, a, b, ini, o0, o1):
        add("v", "scan", (out, a, b, ini, o0, o1), [out], [a, b, ini], cyc(out, a, 1.01))

    def ms(out, v):
        add("v", "ms", (out, v), [out], [], cyc(out, out, 1))

    def act(out, a, fn, bias=None, scale=None):
        add("a", "act", (out, a, fn, bias, scale), [out], [a, bias, scale], cyc(out, a, 1.01))

    def mm(lst):
        c = sum(max(64, width(m[2])) * (4 if dty(m[2]) == F else 1) for m in lst) * cfg["pe"] + 30
        add("p", "mm", lst, [m[0] for m in lst], [m[1] for m in lst] + [m[2] for m in lst], c)

    def group(lst):
        mm([m + (j == 0, j == len(lst) - 1) for j, m in enumerate(lst)])

    def iota(out, pat, base, cm):
        add("g", "iota", (out, pat, base, cm), [out], [], 160 + 2 * width(out))

    def keep(out, a, pat, op, fill, base, cm):
        add("g", "sel", (out, a, pat, op, fill, base, cm), [out], [a], 205 + 2 * width(out))

    nd = [0]

    def dma(q, out, a, nbytes):
        nd[0] += 1
        add(q, "dma", (out, a), [] if out[0] == "hbm" else [out], [] if a[0] == "hbm" else [a],
            2000 + 128 * nbytes / 200.0, sem="d%d" % nd[0])

    def move(src, dst, shift, nbytes, via=False):
        nd[0] += 1
        k = add("g", "rem", (src, dst, shift, "r%d" % nd[0], via), [], [src], 128 * nbytes / cfg["link"], sem="ls")
        ops[k]["pre"] = 2500 + via * (2500 + 128 * nbytes / cfg["hop"])
        ops[k]["cost"] += ops[k]["pre"]
        add("x", "arr", (), [dst], [], 1, sem="r%d" % nd[0], after=k)

    def gather(out, win, off, on):
        act(out, ("ind", win, off), AF.Copy)
        cp(out, ("ind", win, off))
        either(on)

    def scale(out, a, s, on="?"):
        act(out, a, AF.Identity, scale=s)
        ts(out, a, s, None, AL.mult)
        either(on)

    def reach(p):
        return min(S, (K * p // (K + p) + 2 + 15) // 16 * 16)

    dma("s", R("pra", 0, 3), ("hbm", "obs", 0, 3), 12)
    dma("s", C("pra", 3), ("hbm", "eps", 0, 1), 4)
    dma("s", R("b0s", 0, 1024), ("hbm", "b0", 0, 1024), 2048)
    dma("a", R("b0s", 1024, 2048), ("hbm", "b0", 1024, 2048), 2048)
    dma("s", R("f0s", 0, 1024), ("hbm", "f0", 0, 1024), 2048)
    dma("a", R("f0s", 1024, 2048), ("hbm", "f0", 1024, 2048), 2048)
    dma("s", R("pis"), ("hbm", "pi", 0, 256), 1024)
    for j, nm in ((4, "lam"), (5, "rf"), (6, "rb")):
        dma("s", C("pra", j), ("hbm", nm, 0, 1), 4)
    dma("s", R("nza"), ("hbm", "nz", 0, S), 4096)

    rc = C("rc", 0)
    io = R("iod", 0, 128)
    iota(R("iod"), [[1, 144]], 0, -1)
    iota(C("rci", 0), [[1, 1]], 0, 1)
    iota(R("j16"), [[0, 26], [1, 16]], 0, 0)
    iota(R("c16"), [[16, 256]], 0, 0)
    iota(R("nc16"), [[-16, 272]], -16, 0)
    iota(R("mc"), [[16, 256]], int(MG), 0)
    iota(R("ones", 0, 128), [[0, 128]], 1, 0)
    act(R("ones", 128, 512), R("j16", 0, 384), AF.Identity, bias=1.0, scale=0.0)
    iota(R("tbc"), [[16, 17]], 300 - 1024, 0)
    ts(C("rci", 1), C("rci", 0), 15, None, AL.bitwise_and)
    cp(rc, C("rci", 1))
    one = R("ones", 0, 128)
    col, grp = [[1, 128]], [[-16, 8], [0, 16]]

    def ingroup(out, a):
        keep(out, a, grp, AL.is_ge, 0.0, 0, 1)
        keep(out, out, [[16, 8], [0, 16]], AL.is_ge, 0.0, 15, -1)

    def corner(out, v):
        keep(out, out, [[-16, 8], [200, 16]], AL.not_equal, v, 0, 1)

    ts(R("q1"), R("iod"), rc, 15.0, AL.add, AL.is_equal)
    ingroup(R("bo"), one)
    keep(R("tri"), R("bo"), col, AL.is_ge, 0.0, 0, -1)
    ts(R("dmask"), R("j16"), rc, BIG, AL.is_equal, AL.mult)
    scale(R("c16"), R("c16"), 1.0 / K)
    scale(R("bo16"), R("bo"), 16.0)
    scale(R("trk"), R("tri"), float(K))
    rng = []
    for b in range(8):
        p0, p1 = (256 * b + 16) / 2048.0, (b + 1) / 8.0
        rng.append((0 if b == 0 else int(256 * p0 / (2 - p0)) // 2 * 2, min(256, int(512 * p1 / (1 + p1)) // 2 * 2 + 2)))
    z0 = [sum(r[1] - r[0] for r in rng[:b]) - rng[b][0] for b in range(8)]
    cz = [sum(2 if hi <= c else lo <= c and on == "A" for (lo, hi), on in zip(rng, cfg["zc"])) for c in range(256)]
    ends = [c for c in range(256) if c == 0 or cz[c] != cz[c - 1]] + [256]
    for a, b in zip(ends, ends[1:]):
        act(R("cz", a, b), R("iod", 0, b - a), AF.Identity, bias=float(cz[a]), scale=0.0)
    scale(R("boh"), R("bo"), 0.5)
    scale(R("bo8"), R("bo"), 8.0)
    for x in "fb":
        iota(C("o" + x, 0), [[0, 1]], 0, 0)
        iota(R("st" + x, 1024, 1040), [[0, 16]], int(MG) + 5000, 0)
    ts(R("idf"), io, 0.0, None, AL.is_equal)
    scale(R("idb"), R("idf"), 1.0)
    scale(R("idk"), R("idf"), float(K))
    scale(R("nid"), R("idf"), -1.0)
    act(R("w1"), R("j16", 0, 128), AF.Exp, bias=-LN2, scale=-LN2)
    ingroup(R("w1"), R("w1"))
    scale(R("nw1"), R("w1"), -1.0)
    keep(R("b0"), one, grp, AL.is_equal, 0.0, 0, 1)
    act(R("dl"), R("j16", 0, 128), AF.Exp, bias=-2 * LN2, scale=-LN2)
    keep(R("dl"), R("dl"), grp, AL.is_equal, 0.0, -1, 1)
    keep(R("dl"), R("dl"), grp, AL.not_equal, -0.5, 0, 1)
    scale(R("gg"), R("tri"), -1.0)
    keep(R("gg"), R("gg"), col, AL.not_equal, -2.0, 0, -1)
    keep(R("gg"), R("gg"), grp, AL.not_equal, 1.0, 0, 1)
    corner(R("gg"), 0.0)
    scale(R("nb0"), R("b0"), -1.0)
    scale(R("bk"), R("b0"), 1024.0)
    scale(R("bo512"), R("bo"), PB / 16)
    keep(R("stt"), R("bo"), col, AL.is_gt, 0.0, 0, -1)
    keep(R("str"), R("stt"), col, AL.not_equal, 64.0, 0, -1)
    ms(C("po", 0), -7.5)
    scale(R("pb0"), R("bo"), 2.0)
    keep(R("pb0"), R("pb0"), col, AL.is_equal, 0.0, 1, -1)
    keep(R("pb0"), R("pb0"), col, AL.not_equal, -1.0, 0, -1)
    for j in range(1, 5):
        scale(R("pb%d" % j), R("pb0"), 2.0 ** j if j < 4 else PB)
    for j in range(4):
        ts(C("rci", 2 + j), C("rci", 1), j, 1, AL.arith_shift_right, AL.bitwise_and)
    cp(R("rc", 4, 8), R("rci", 2, 6))
    for j in range(4):
        scale(R("wb%d" % j), R("w1"), C("rc", 4 + j))
    keep(R("shb"), one, col, AL.is_equal, 0.0, -16, -1)
    keep(R("shb"), R("shb"), col, AL.not_equal, 1.0, 112, -1)
    scale(R("shf"), R("shb"), 1.0)
    ts(C("rc", 2), C("rc", 4), float(WB - 1 - WF), float(WF), AL.mult, AL.add)
    tt(C("rc", 3), C("rc", 2), rc, AL.add)
    ts(C("rc", 8), rc, -6.5, 2 * PB, AL.add, AL.mult)
    ts(C("rc", 9), C("rc", 3), -1.0, 16.0, AL.mult, AL.add)
    ts(R("nfill"), R("nc16", 0, 256), C("rc", 9), None, AL.add)
    ts(R("tbc"), R("tbc"), rc, 16.0, AL.add, AL.mult)
    ts(R("eg"), R("iod", 0, 136), 2.0, rc, AL.mult, AL.add)
    ts(R("ef"), R("eg"), 16.0, -1.0, AL.is_equal, AL.mult)
    ts(R("eg"), R("eg"), 15.0, -1.0, AL.is_equal, AL.mult)
    for r, v in ((R("win", 0, 16), 0), (C("nn", 0), -8), (R("nn", 256, 280), -8), (R("ok", 256, 258), 1), (R("ok", 257, 272), 0)):
        iota(r, [[0, width(r)]], v, 0)
    cp(R("pia"), R("pis"))
    move(R("pra", 0, 7), R("prb", 0, 7), -1, 28)
    move(R("pra", 0, 4), R("prc", 0, 4), 1, 16)
    move(R("pra", 0, 4), R("prd", 0, 4), -2, 16)
    move(R("pia"), R("pib"), -1, 512)
    move(R("nza"), R("nzb"), -1, 4096)
    for x in "abcd":
        scale(R("pn" + x, 0, 4), R("pr" + x, 0, 4), -1.0)
        scale(C("pn" + x, 4), C("pr" + x, 3), -SC)

    def sel(i):
        return R("q1", 15 - i, 143 - i)

    def ancestors(t, x, pool, par, res):
        pr, pn = "pr" + par, "pn" + par
        bank, bk2 = ("ps4", "ps5") if x == "b" else ("ps6", "ps7")
        m0 = S if x == "b" else 0
        how = cfg["hit"][t][x]
        cw = S // len(how)
        for k, h in enumerate(how):
            a, b = k * cw, (k + 1) * cw
            src = [R("mw", m0 + a, m0 + b)]
            if h == "D":
                ts(src[0], R(pool, a, b), C(pr, t), C(pr, 3), AL.subtract, AL.is_gt)
                src.append(R("hit", m0 + a, m0 + b))
                ts(src[1], R(pool, a, b), C(pr, t), C(pn, 3), AL.subtract, AL.is_lt)
            else:
                aw = R("ab", m0 + a, m0 + b)
                act(aw, R(pool, a, b), AF.Abs, bias=C(pn, t))
                act(src[0], aw, AF.Relu, bias=C(pn, 4), scale=SC)
                ts(src[0], aw, C(pr, 3), None, AL.is_gt)
                either(h)
            group([(R(bank, a // 16, b // 16), sel(i), (s[0], s[1] + i, s[2], 16)) for s in src for i in range(16)])
        w, o, tq = R("w" + x), "o" + x, "tq" + x
        tot = C(o, 128)
        ts(w, R(bank, 0, 128), 0.0, 1.0, AL.is_le, AL.add)
        group([(R(bank, 128, 256), R("bo"), w)])
        scan(R(o, 1, 129), R(bank, 128, 256), R("nc16", 0, 128), 0.0, AL.add, AL.max)
        cc = R(bank, 256, 384)
        group([(cc, R("idk"), R(o, 0, 128)), (cc, R("trk"), w)])
        y, out = R(bank, 0, 256), R(bk2, 0, 256)
        mm([(y, R("dl"), R("ones", 0, 256), True, False)])
        scan(R("ec" + x), R("dmask", 0, 128), R(o, 1, 129), 0.0, AL.add, AL.min)
        mm([(R(bk2, 256, 512), R("boh"), R("cz"), True, False)])
        if "A" in cfg["zc"]:
            act(R("en" + x), R("ec" + x, 15, 128, 16), AF.Identity, bias=1.0 / 512, scale=-1.0)
        seq = sorted(range(8), key=lambda b: (cfg["zc"][:b].count(cfg["zc"][b]), cfg["zc"][b] == "A"))
        for b in seq:
            lo, hi = rng[b]
            z = R("zc" + x, z0[b] + lo, z0[b] + hi)
            if cfg["zc"][b] == "A":
                act(z, R("c16", lo, hi), AF.Sign, bias=C("en" + x, b), scale=tot)
            else:
                ts(z, R("c16", lo, hi), tot, C("ec" + x, 16 * b + 15), AL.mult, AL.is_ge)
            mm([(R(bk2, 256 + lo, 256 + hi), R("boh" if cfg["zc"][b] == "A" else "bo"), z, False, b == seq[-1])])
        add("v", "rcp", (C(tq, 1), tot), [C(tq, 1)], [tot], 250)
        act(R("qm" + x), cc, AF.Identity, bias=MG, scale=C(tq, 1))
        ts(R("qm" + x), cc, C(tq, 1), MG, AL.mult, AL.add)
        either(cfg["qm"])
        ts(R("qt" + x), R("qm" + x), -MG, tot, AL.add, AL.mult)
        tt(R(bank, 384, 512), cc, R("qt" + x), AL.is_gt)
        tt(R("st" + x, 0, 1024, 8), R(bank, 384, 512), R("qm" + x), AL.add)
        scan(R("eb" + x), R("dmask", 0, 256), R(bk2, 256, 512), 0.0, AL.add, AL.min)
        mm([(out, R("bo8"), R("cz"), True, False)]
           + [(R(bk2, lo, hi), R("bo8" if cfg["zc"][b] == "A" else "bo16"), R("zc" + x, z0[b] + lo, z0[b] + hi), False, False)
              for b, (lo, hi) in enumerate(rng)])
        ts(R("l2" + x), R("eb" + x, 15, 256, 16), 8.0, None, AL.mult)
        for h in range(2):
            a, b = 256 * h, 256 * h + 256
            tt(R("x12" + x, a, b), ("ind", R("st" + x, 8 * h, 8 * h + 1032), R("l2" + x)), R("mc"), AL.subtract)
            ts(R("xc" + x, a, b), R("x12" + x, a, b), 0.0, 16.0, AL.max, AL.min)
            act(R("xe" + x, a, b), R("xc" + x, a, b), AF.Exp, scale=LN2)
            if h == 0:
                ts(R("p0" + x), R("x12" + x, 0, 256), 0.0, None, AL.is_le)
                act(R("p0" + x), R("xc" + x, 0, 256), AF.Relu, bias=1.0, scale=-1.0)
                either(cfg["p0"])
                mm([(y, R("nw1"), R("p0" + x), False, False), (out, R("bo"), R("p0" + x), False, False)])
            mm([(y, R("w1"), R("xe" + x, a, b), False, h == 1)])
        ts(R("xf" + x), y, MG, MG, AL.add, AL.subtract)
        mm([(out, R("gg"), R("xf" + x), False, True)])
        cp(R(res), out)

    def filling(t, j, a, b):
        e = b + 16 * (b == 256)
        w, v = b - a, e - a
        pb = "ps5" if j % 2 else "ps6"
        arg, xr, n0 = R(pb, 2 * v, 2 * v + w), R("ps7", 256, 256 + v), R("ps7", 0, v + 1)
        ts(R("ok", a, b), R("ps4", a, b), 7.5, None, AL.is_le)
        group([(R(pb, 0, v), R("bo"), R("ok", a, e))])
        scan(R("po", a + 1, e + 1), R(pb, 0, v), R("nc16", 0, v), C("po", a), AL.add, AL.max)
        group([(n0, R("idf"), R("po", a, e + 1)), (R("ps7", 0, v), R("stt"), R("ok", a, e))])
        mm([(arg, R("idf"), R("po", a, b), True, False), (arg, R("str"), R("ok", a, b), False, False)])
        ts(R("f16", a, e + 1), n0, M16, M16, AL.add, AL.subtract)
        mm([(arg, R("nid"), R("f16", a, b), False, True)])
        act(R("ee", a, b), arg, AF.Exp, bias=LN2 * (8.5 - 64), scale=LN2)
        group([(xr, R("idf"), R("po", a, e)), (xr, R("nb0"), R("f16", a, e))])
        for h in range(0, 5 * w, 512):
            top = min(5 * w, h + 512)
            mm([(R("psb", h, top), R("dl"), R("ones", 0, top - h), True, False)])
            lst = []
            for k, mat in enumerate(("wb0", "wb1", "wb2", "wb3", "w1")):
                lo, hi = max(h, k * w), min(top, k * w + w)
                if lo < hi:
                    lst.append((R("psb", lo, hi), R(mat), R("ee", a + lo - k * w, a + hi - k * w), False, hi == top))
            mm(lst)
            ts(R("ff", 5 * a + h, 5 * a + top), R("psb", h, top), MG, MG, AL.add, AL.subtract)
        s1, s2, pg = R(pb, 0, v), R(pb, v, 2 * v), R(pb, 2 * v, 3 * v)
        group([(s1, R("bk"), R("f16", a, e)), (s1, R("b0"), R("f16", a, e))])
        group([(s2, R("bk"), R("f16", a + 1, e + 1))])
        act(pg, xr, AF.Relu, bias=C("rc", 8), scale=-2 * PB)
        if e > b:
            ts(C("nn", 257), C(pb, v + w - 1), -1.0 / 1024, C("rc", 3), AL.mult, AL.subtract)
        scan(R("pe", 2 * a, 2 * e), R("dmask", 0, 2 * v), R(pb, 0, 2 * v), 0.0, AL.add, AL.min)
        q, q2 = R("pq", a // 16, e // 16), R("pq2", a // 16, e // 16)
        tt(q, R("pe", 2 * a + 15, 2 * a + v, 16), R("pe", 2 * a + v + 15, 2 * e, 16), AL.subtract)
        tt(q2, q, R("tbc", a // 16, e // 16), AL.min)
        ts(R("pl", a // 16, e // 16), q2, 1.0 / 16, 1024.0, AL.mult, AL.add)
        arg = R(pb, 0, w)
        mm([(arg, R("idb"), R("nc16", a, b), True, False), (arg, R("bo512"), R("ones", 0, w), False, False)])
        for k in range(5):
            mm([(arg, R("pb%d" % k), R("ff", 5 * a + k * w, 5 * a + (k + 1) * w), False, k == 4)])
        scan(R("nn", a + 1, b + 1), arg, R("dmask", 0, w), C("nn", a), AL.min, AL.min)
        tt(R("yy", a, e), R("nn", a, e), pg, AL.subtract)
        tt(("ind", R("pw"), R("pl", a // 16, e // 16)), R("nn", a + 1, e + 1), R("yy", a, e), AL.max)

    pools = [{"f": "f0s", "b": "b0s"}, {"f": "fp1", "b": "lb"}, {"f": "lf", "b": "lb"}]
    dest = [{"f": "fp1", "b": "sb0"}, {"f": "sf1", "b": "lb"}, {"f": "fp1", "b": "lb"}]
    ub = [("psa", 0), ("psa", 512), ("psb", 0), ("psb", 512)]
    for t in range(3):
        par = "b" if t == 1 else "a"
        pr, pn = "pr" + par, "pn" + par
        bias[0] = 0.0
        dma("s", R("pw", 0, 256), R("nfill"), 1024)
        al = {"f": "laf" if t == 2 else "alf", "b": "lab" if t == 1 else "alb"}
        for x in cfg["order"][t]:
            bias[0] = cfg["bb"][t] if x == "b" else cfg["bf"][t]
            if al[x][0] == "a":
                ancestors(t, x, pools[t][x], par, al[x])
            else:
                ancestors(t, x, dest[t - 1][x], "c" if t == 1 else "d", "sa" + x)
                move(R("sa" + x), R(al[x]), -2 if t == 1 else 2, 512)
        bias[0] = 0.0
        cw = K // len(cfg["bA"][t])
        bias[0] = cfg["ba"][t]
        for k, on in enumerate(cfg["bA"][t]):
            a, b = k * cw, (k + 1) * cw
            gather(R("win", WB + a, WB + b), R(pools[t]["b"], 0, reach(b)), R(al["b"], a // 16, b // 16), on)
        bias[0] = 0.0
        a = done = 0
        for k, cw in enumerate(cfg["gch"][t]):
            b = a + cw
            bias[0] = cfg["slope"] * (K - a)
            gather(R("win", WF + a, WF + b), R(pools[t]["f"], 0, reach(b)), R(al["f"], a // 16, b // 16), cfg["fi"][t][k])
            tt(R("dd", a, b), ("ind", R("win", WB, WW), R("pi" + par, a // 16, b // 16)), R("win", WF + a, WF + b), AL.subtract)
            for c in range(a, b, 512):
                c1 = min(b, c + 512)
                e = R("psa", c % 1024, c % 1024 + c1 - c)
                scale(e, R("dd", c, c1), C(pr, 4), "A")
                tt(R("win", WM + c, WM + c1), R("win", WF + c, WF + c1), e, AL.add)
            act(R("ab", a, b), R("win", WM + a, WM + b), AF.Abs, bias=C(pn, t))
            if cfg["acc"][t][k] == "V":
                ts(R("hit", a, b), R("ab", a, b), C(pr, 3), None, AL.is_gt)
            else:
                act(R("hit", a, b), R("ab", a, b), AF.Relu, bias=C(pn, 4), scale=SC)
                act(R("hit", a, b), R("hit", a, b), AF.Sign)
                ts(R("hit", a, b), R("hit", a, b), 0.0, None, AL.is_gt)
                either("A" if cfg["acc"][t][k] == "A" else "V")
            if b - done >= 1024 or b // 16 in cfg["parts"][t]:
                group([(R("ps4", done // 16, b // 16), sel(i), R("hit", done + i, b, 16)) for i in range(16)])
                done = b
            if t == 2:
                bias[0] = cfg["ye"]
                act(R("tb", a, b), R("dd", a, b), AF.Square)
                act(R("tb", a, b), R("tb", a, b), AF.Exp, scale=-1.0)
                for z in range(a, b, 256):
                    mm([(R("psb", 512, 768), R("idf"), R("tb", z, z + 256), z == 0, z == K - 256)])
                bias[0] = 0.0
            parts = cfg["parts"][t]
            if b // 16 in parts:
                j = parts.index(b // 16)
                bias[0] = cfg["bp"][j]
                filling(t, j, parts[j - 1] if j else 0, b // 16)
                bias[0] = 0.0
            a = b
        if t == 2:
            act(R("yes"), R("psb", 512, 768), AF.Copy)
            dma("s", ("hbm", "ye", 0, 256), R("yes"), 1024)
        seq = cfg["step"][t]
        for x in (seq[0], "f" if seq[0] == "b" else "b"):
            j = 0 if x == "f" else 1
            mat = "eg" if j else "ef"
            for a, b in (((0, 64), (64, 128)) if x == seq[0] else ((0, 128),)):
                u = R(("ps6", "ps7", "ps4")[(a > 0) + 2 * (x != seq[0])], a, b)
                group([(u, R(mat, 8, 136), R("pw", 2 * a, 2 * b, 2)), (u, R(mat, 0, 128), R("pw", 2 * a + 1, 2 * b, 2))])
                cp(R("ll", 128 * j + a, 128 * j + b), u)
        pos = {"f": 0, "b": 0}
        nb = 0
        for x in seq:
            j = 0 if x == "f" else 1
            sa = sum(cfg["sch"][t][:pos[x]])
            bias[0] = cfg["s" + x][t] + cfg["slope2"] * (S - sa)
            cw = cfg["sch"][t][pos[x]]
            sb = sa + cw
            pos[x] += 1
            a, b = j * S + sa, j * S + sb
            src = ("ind", R("win"), R("ll", a // 16, b // 16))
            act(R("ab", a, b), src, AF.Square)
            tt(R("dd", a, b), src, R("ab", a, b), AL.subtract)
            mat = "sh" if x == "b" and t < 2 else "id"
            if cw > 512 and nb % 2:
                nb += 1
            un, u0 = ub[nb % 4]
            cuts = [(c, min(cw, c + 512)) for c in range(0, cw, 512)]
            nb += len(cuts)
            if mat == "sh":
                scale(R("tb", a, b), R("dd", a, b), C(pr, 5 + j), "A")
                for c, c1 in cuts:
                    u = R(un, u0 + c, u0 + c1)
                    group([(u, R("shf"), R("tb", a + c, a + c1)), (u, R("shb"), R("nz" + par, sa + c, sa + c1))])
            else:
                mm([(R(un, u0 + c, u0 + c1), R("idb"), R("ones", 0, c1 - c), True, False) for c, c1 in cuts])
                scale(R(un, u0, u0 + cw), R("dd", a, b), C(pr, 5 + j), "A")
                mm([(R(un, u0 + c, u0 + c1), R("idb"), R("nz" + par, sa + c, sa + c1), False, True) for c, c1 in cuts])
            new = R(dest[t][x], sa, sb)
            ts(new, R(un, u0, u0 + cw), 0.0, 1.0, AL.max, AL.min)
            if t == 2:
                dma("s", ("hbm", "y" + x, sa, sb), new, 4 * cw)
            elif x == "bf"[t]:
                way = cfg["way"][t][pos[x] - 1]
                mid = {"D": sb, "R": sa, "S": (sa + sb) // 2}[way]
                for c, c1, via in ((mid, sb, True), (sa, mid, False)):
                    if c < c1:
                        move(R(dest[t][x], c, c1), R("l" + x, c, c1), 4 * t - 2, 4 * (c1 - c), via)
    return ops


def banks(a):
    return range(PS[a[0]][1] + a[1] // 512, PS[a[0]][1] + (a[2] - 1) // 512 + 1)


def prepare(cfg):
    ops = declare(cfg)
    n = len(ops)
    acc = {}
    last = {}
    for i, o in enumerate(ops):
        dep = set() if o["after"] is None else {o["after"]}
        for lst, wr in ((o["rd"], False), (o["wr"], True)):
            for a in lst:
                for (j, c0, c1, w) in acc.get(a[0], []):
                    if (w or wr) and c0 < a[2] and a[1] < c1:
                        dep.add(j)
        bk = set(b for a in o["rd"] + o["wr"] if a[0] in PS for b in banks(a))
        for b in bk:
            prev, cur = last.get(b, ([], []))
            if cur and (ops[cur[-1]]["eng"] != o["eng"] or ops[cur[-1]]["alt"] or o["alt"]):
                prev, cur = cur, []
            dep.update(prev)
            if cur and o["eng"] == "p":
                dep.add(cur[-1])
            last[b] = (prev, cur + [i])
        for lst, wr in ((o["rd"], False), (o["wr"], True)):
            for a in lst:
                if wr:
                    acc[a[0]] = [e for e in acc.get(a[0], []) if not (a[3] == 1 and a[1] <= e[1] and e[2] <= a[2])]
                acc.setdefault(a[0], []).append((i, a[1], a[2], wr))
        dep.discard(i)
        o["dep"] = dep
    succ = [[] for _ in range(n)]
    for i, o in enumerate(ops):
        for j in o["dep"]:
            succ[j].append(i)
    pri = [0.0] * n
    for i in range(n - 1, -1, -1):
        pri[i] = ops[i]["cost"] + max([pri[j] + cfg["lat"] for j in succ[i]], default=0.0)
    return ops, succ, [p + o["bias"] for p, o in zip(pri, ops)]


def schedule(cfg, ops, succ, pri):
    n = len(ops)
    free = dict((e, 0.0) for e in "vapgsx")
    link = [0.0, 0.0]
    done, start, took = [0.0] * n, [0.0] * n, [False] * n
    left = [len(o["dep"]) for o in ops]
    at = [0.0] * n
    ready = dict((e, {}) for e in "vapgsx")

    def offer(i):
        o = ops[i]
        ready[o["eng"]][i] = pri[i]
        if o["alt"]:
            ready[o["alt"][0]][i] = pri[i] - cfg["p" + o["alt"][0]]

    for i in range(n):
        if left[i] == 0:
            offer(i)
    order = []
    while len(order) < n:
        best = None
        for e in "vapgsx":
            c = ready[e]
            if c:
                t0 = max(free[e], min(at[i] for i in c))
                p, i = max((c[i], -i) for i in c if at[i] <= t0 + 1)
                p2, i2 = max((c[j], -j) for j in c if at[j] <= t0 + 1 + min(cfg["wait"], 0.5 * ops[-i]["cost"]))
                if p2 > p + cfg["gap"]:
                    t0, i = at[-i2], i2
                key = (t0, ops[-i]["eng"] != e)
                if best is None or key < best[0]:
                    best = (key, -i, e)
        (t0, alt), i, e = best
        o = ops[i]
        took[i] = alt
        ready[o["eng"]].pop(i, None)
        if o["alt"]:
            ready[o["alt"][0]].pop(i, None)
        if o["kind"] == "dma":
            free[e] = t0 + 60; done[i] = t0 + o["cost"]
        elif o["kind"] == "rem":
            free[e] = t0 + 500
            via = o["args"][4]
            done[i] = link[via] = max(link[via], t0 + o["pre"]) + o["cost"] - o["pre"]
        else:
            done[i] = free[e] = t0 + (o["alt"][3] if alt else o["cost"])
        start[i] = t0
        order.append(i)
        for j in succ[i]:
            left[j] -= 1
            at[j] = max(at[j], done[i] + (0 if e == "p" == ops[j]["eng"] else cfg["lat"]))
            if left[j] == 0:
                offer(j)
    return order, took, start, done


def justify(cfg, ops, succ, done):
    n = len(ops)
    shape = []
    for o in ops:
        if o["kind"] == "dma":
            shape.append((o["eng"], 0.0, 60.0, o["cost"] - 60))
        elif o["kind"] == "rem":
            shape.append(("link%d" % o["args"][4], o["pre"], o["cost"] - o["pre"], 0.0))
        else:
            shape.append((o["eng"], 0.0, 0.0 if o["eng"] == "x" else o["cost"], 1.0))

    def place(key, before, back):
        start, end, busy = [0.0] * n, [0.0] * n, {}
        for i in sorted(range(n), key=lambda i: (-key[i], -i if back else i)):
            res, pre, dur, post = shape[i]
            if back:
                pre, post = post, pre
            t = pre + max([end[j] + (0 if res == "p" == shape[j][0] else cfg["lat"]) for j in before[i]], default=0.0)
            lst = busy.setdefault(res, [])
            k = len(lst)
            while k and lst[k - 1][1] > t:
                k -= 1
            while k < len(lst) and lst[k][0] < t + dur:
                t = max(t, lst[k][1]); k += 1
            lst.insert(k, (t, t + dur))
            start[i], end[i] = t - pre, t + dur + post
        return start, end

    best = None
    for _ in range(cfg["passes"]):
        start, done = place(place(done, succ, True)[1], [o["dep"] for o in ops], False)
        if best is None or max(done) < max(best[1]):
            best = (start, done)
    return sorted(range(n), key=lambda i: (best[0][i], i)), best[0], best[1]


def plan(cfg):
    ops, succ, pri = prepare(cfg)
    order, took, start, done = schedule(cfg, ops, succ, pri)
    for i, o in enumerate(ops):
        if took[i]:
            o["eng"], o["kind"], o["args"], o["cost"] = o["alt"]
    if cfg["passes"]:
        order, start, done = justify(cfg, ops, succ, done)
    for i, o in enumerate(ops):
        o["took"], o["t0"], o["t1"] = took[i], start[i], done[i]
    count = dict((e, 0) for e in "vapg")
    known = dict((e, {}) for e in "vapgsx")
    for i in order:
        o = ops[i]
        kn = known[o["eng"]]
        o["wait"] = []
        need = {}
        for j in o["dep"]:
            p = ops[j]
            if o["eng"] == "x" or (p["eng"] == "p" and o["eng"] == "p"):
                continue
            if kn.get(p["tag"][0], 0) < p["tag"][1] and need.get(p["tag"][0], (0,))[0] < p["tag"][1]:
                need[p["tag"][0]] = (p["tag"][1], j)
        for s in sorted(need, key=lambda s: -done[need[s][1]]):
            val, j = need[s]
            if kn.get(s, 0) >= val:
                continue
            o["wait"].append((s, val))
            for s2, v2 in ops[j]["clock"].items():
                kn[s2] = max(kn.get(s2, 0), v2)
        o["inc"] = False
        if o["kind"] == "dma":
            o["tag"] = (o["sem"], 16)
        elif o["kind"] in ("arr", "rem"):
            o["tag"] = (o["sem"], 1)
        else:
            o["inc"] = bool(succ[i])
            if o["inc"]:
                count[o["eng"]] += o["n"]
            o["tag"] = ("c" + o["eng"], count[o["eng"]])
        o["clock"] = {} if o["eng"] == "x" else dict(kn)
        o["clock"][o["tag"][0]] = o["tag"][1]
    return ops, order, count


OPS, ORDER, COUNT = plan(CFG)
SEMAPHORES = ["cv", "ca", "cp", "cg", "ls"] + [o["sem"] for o in OPS if o["kind"] in ("dma", "arr")]


def rank_program(g, core, T, topo):
    def ap(a):
        if not isinstance(a, tuple):
            return a
        if a[0] == "ind":
            return ap(a[1]).indirect(ap(a[2]))
        if a[0] == "hbm":
            return T[a[1]][:] if a[3] - a[2] == T[a[1]].shape[1] else T[a[1]][:, a[2]:a[3]]
        return T[a[0]][:, a[1]:a[2]] if a[3] == 1 else T[a[0]][:, a[1]:a[2]:a[3]]

    def helper(r):
        c = T.cores[r]
        far = [T.cores[(r + o["args"][2]) % N] for o in OPS if o["kind"] == "rem" and o["args"][4]]
        return [h for h in topo.cores_of(c) if topo.die(h) != topo.die(c) and T.rank_of(h) is None
                and all(topo.may_write(h, d) for d in far)][0]

    def spare(r, dst):
        c = T.cores[r]
        return [e for e in topo.engines(c, helper(r)) if e not in topo.engines(c, dst)]

    rank = T.rank_of(core)
    if rank is None:
        sent = 0
        for r in range(N):
            if helper(r) == core:
                for i in ORDER:
                    a = OPS[i]["args"]
                    if OPS[i]["kind"] == "rem" and a[4]:
                        dst = T.cores[(r + a[2]) % N]
                        rid, pid, _ = topo.addr(dst)
                        g.wait_ge(T.sem[a[3]], len(spare(r, dst)))
                        g.remote_dma(ap(a[1]), ap(a[1]), T.sem[a[3]], T.sem.ls, pid, rid, topo.mask(core, dst))
                        sent += len(topo.engines(core, dst))
        if sent:
            g.wait_ge(T.sem.ls, sent)
        return
    q = {"v": g.vector, "a": g.scalar, "p": g.tensor, "g": g, "s": g.sync}
    arrive = {}
    for o in OPS:
        if o["kind"] == "rem":
            src = (rank - o["args"][2]) % N
            arrive[o["args"][3]] = len(topo.engines(helper(src) if o["args"][4] else T.cores[src], core))
    sent = 0
    for i in ORDER:
        o = OPS[i]
        if o["eng"] == "x":
            continue
        e, k, a = q[o["eng"]], o["kind"], o["args"]
        for s, val in o["wait"]:
            e.wait_ge(T.sem[s], arrive.get(s, val))
        if k == "rem":
            dst = T.cores[(rank + a[2]) % N]
            use = spare(rank, dst) if a[4] else topo.engines(core, dst)
            rid, pid, _ = topo.addr(helper(rank) if a[4] else dst)
            g.remote_dma(ap(a[1]), ap(a[0]), T.sem[a[3]], T.sem.ls, pid, rid, sum(1 << x for x in use))
            sent += len(use)
            continue
        if k == "dma":
            e.dma_start(ap(a[0]), ap(a[1])).then_inc(T.sem[o["sem"]], 16)
            continue
        if k == "mm":
            ins = [e.matmul(ap(m[0]), ap(m[1]), ap(m[2]), m[3], m[4]) for m in a]
        elif k == "ts":
            ins = [e.tensor_scalar(*[ap(x) for x in (a if a[5] is not None else a[:5])])]
        elif k == "tt":
            ins = [e.tensor_tensor(ap(a[0]), ap(a[1]), ap(a[2]), a[3])]
        elif k == "cp":
            ins = [e.tensor_copy(ap(a[0]), ap(a[1]))]
        elif k == "scan":
            ins = [e.tensor_tensor_scan(*[ap(x) for x in a])]
        elif k == "ms":
            ins = [e.memset(ap(a[0]), a[1])]
        elif k == "rcp":
            ins = [e.reciprocal(ap(a[0]), ap(a[1]))]
        elif k == "sel":
            ins = [e.affine_select(ap(a[0]), ap(a[1]), *a[2:])]
        elif k == "iota":
            if dty(a[0]) == I:
                ins = [e.iota(ap(a[0]), a[1], a[2], a[3])]
            else:
                ins = [e.iota(ap(a[0]), a[1], a[2], a[3], allow_small_or_imprecise_dtypes=True)]
        else:
            kw = {}
            if a[3] is not None:
                kw["bias"] = ap(a[3])
            if a[4] is not None:
                kw["scale"] = ap(a[4])
            ins = [e.activation(ap(a[0]), ap(a[1]), a[2], **kw)]
        if o["inc"]:
            for x in ins:
                x.then_inc(T.sem["c" + o["eng"]], 1)
    for x in "vapg":
        g.wait_ge(T.sem["c" + x], COUNT[x])
    g.wait_ge(T.sem.ls, sent)
    for o in OPS:
        if o["kind"] == "dma":
            g.wait_ge(T.sem[o["sem"]], 16)
        elif o["kind"] == "arr":
            g.wait_ge(T.sem[o["sem"]], arrive[o["sem"]])
